import numpy as np, ml_dtypes
CORES = [50,52,122,124]
N = 4
import mx_ref
NC = 128
A = np.float32(0.0125)
BF = ml_dtypes.bfloat16
def cut(t, i, w=512):
    return t[:, w * i:w * i + w]
def tile(rs):
    return np.stack(rs, axis=2).reshape(128, -1).astype(BF)
def setup_inputs(rng):
    def f(*shape):
        return mx_ref.flush((rng.standard_normal(shape, dtype=np.float32) * np.exp2(rng.integers(-2, 3, shape[:-1] + (1,)))).astype(BF))
    return {"q": f(N, 128, 4 * NC), "k": f(N, 128, 4 * 512), "v": f(N, 128, 512)}
def setup_inputs_blocks(rng):
    d = setup_inputs(rng)
    for k in ("v",): d[k] = mx_ref.spread(d[k], rng, 4)
    for k in ("q", "k"): d[k] = mx_ref.spread(d[k], rng, 1)
    return d
def setup_inputs_wide(rng):
    d = setup_inputs(rng)
    for k in ("v",): d[k] = mx_ref.flush((d[k].astype(np.float32) * np.exp2(rng.integers(-8, 9, (N, 1, 1))).astype(np.float32)).astype(BF))
    return d
def setup_inputs_sharp(rng):
    d = setup_inputs(rng); v = d["q"].astype(np.float32).reshape(N, 128, -1, 4)
    d["q"] = mx_ref.flush((v * np.exp2(rng.integers(-2, 4, (N, 1, v.shape[2], 1))).astype(np.float32)).reshape(d["q"].shape).astype(BF))
    return d
def setup_inputs_far(rng):
    d = setup_inputs(rng); d["q"] = (d["q"].astype(np.float32) * 10).astype(BF)
    return d
def setup_inputs_faroff(rng):
    d = setup_inputs(rng); v = d["k"].astype(np.float32).reshape(N, 128, -1, 4)
    d["k"] = mx_ref.flush((v + 192 * rng.standard_normal((1, 128, 1, 4), dtype=np.float32)).reshape(d["k"].shape).astype(BF))
    return d
def reference(q, k, v, own=None):
    ONE = mx_ref.quantize(np.ones((128, 512), BF))
    K = [[mx_ref.quantize(cut(k[j], b)) for b in range(4)] for j in range(N)]; V = [mx_ref.quantize(v[j]) for j in range(N)]
    Q = [mx_ref.quantize(q[i]) for i in range(N)]
    lo = np.zeros((N, N, NC), np.float32); w = lo.copy(); wlo = lo.copy(); whi = lo.copy(); p = np.zeros((N, N, 128, 4 * NC), BF); o = np.zeros((N, 128, NC), np.float32)
    S = [[[mx_ref.matmul(K[j][b], Q[i]) * A for b in range(4)] for i in range(N)] for j in range(N)]
    for j in range(N):
        lo[j] = [np.max(s, axis=(0, 1)) for s in S[j]]
    hi = np.broadcast_to(lo.max(axis=0) + 8, lo.shape).copy()
    c = lo if own is None else own["c"]
    for j in range(N):
        for i in range(N):
            p[j][i] = tile([np.exp(np.maximum(s - c[j][i], -20).astype(np.float64)).astype(np.float32) for s in S[j][i]])
    use = p if own is None else own["p"]
    for i in range(N):
        e = np.exp((c[:, i] - c[:, i].max(axis=0)).astype(np.float64)); wlo[i] = e * (1 - 4e-5); whi[i] = e * (1 + 4e-5)
        w[i] = e if own is None else own["w"][i]
        num = den = 0
        for j in range(N):
            P = mx_ref.quantize(use[j][i])
            num = num + w[i][j].astype(np.float64) * mx_ref.matmul(V[j], P); den = den + w[i][j].astype(np.float64) * mx_ref.matmul(ONE, P)
        o[i] = (num / den).astype(np.float32)
    return {"c": c, "c__lo": lo, "c__hi": hi, "p": p, "w": w, "w__lo": wlo, "w__hi": whi, "o": o}

@@ -1,0 +1,343 @@
+import numpy as np
+from concourse.bass import DstId, RemoteDMATransfer
+from concourse.mybir import dt, AluOpType, AxisListType, ActivationFunctionType
+
+F = "float32"
+B = "bfloat16"
+C4 = "float8_e4m3fn_x4"
+U8 = "uint8"
+SCRATCH = {
+    "qt": ("sbuf", [128, 512], B), "kt": ("sbuf", [128, 2048], B), "vt": ("sbuf", [128, 512], B),
+    "ot": ("sbuf", [128, 512], B),
+    "qc": ("sbuf", [128, 512], C4), "qx": ("sbuf", [128, 512], U8),
+    "kc": ("sbuf", [128, 512], C4), "kx": ("sbuf", [128, 512], U8),
+    "vc": ("sbuf", [128, 128], C4), "vx": ("sbuf", [128, 128], U8),
+    "oc": ("sbuf", [128, 128], C4), "ox": ("sbuf", [128, 128], U8),
+    "pc": ("sbuf", [128, 512], C4), "px": ("sbuf", [128, 512], U8),
+    "cn": ("sbuf", [128, 32], F), "ct": ("sbuf", [128, 32], F), "cu": ("sbuf", [128, 32], F),
+    "r0": ("sbuf", [128, 16], F), "r1": ("sbuf", [128, 16], F), "r2": ("sbuf", [128, 16], F),
+    "lt": ("sbuf", [128, 512], F),
+    "fx": ("sbuf", [128, 136], F), "fy": ("sbuf", [128, 136], F),
+    "cyb": ("sbuf", [128, 8], F), "cyl": ("sbuf", [128, 8], F),
+    "mask": ("sbuf", [128, 512], F), "zw": ("sbuf", [128, 512], F), "wb": ("sbuf", [128, 512], F),
+    "wr": ("sbuf", [128, 512], F), "zr": ("sbuf", [128, 128], F), "rb": ("sbuf", [128, 128], F),
+    "rw": ("sbuf", [128, 128], F), "dd": ("sbuf", [128, 16], F), "tiny": ("sbuf", [128, 64], F),
+    "num": ("sbuf", [128, 1024], F), "res": ("sbuf", [128, 128], F),
+    "ps0": ("psum", [128, 2048], F), "ps1": ("psum", [128, 2048], F),
+}
+for _k in range(4):
+    SCRATCH["p%d" % _k] = ("sbuf", [128, 512], B)
+    SCRATCH["st%d" % _k] = ("sbuf", [128, 136], F)
+    if _k < 2:
+        SCRATCH["t1_%d" % _k] = ("sbuf", [128, 512], F)
+        SCRATCH["et%d" % _k] = ("sbuf", [128, 512], B)
+    if _k:
+        SCRATCH["al%d" % _k] = ("sbuf", [128, 136], F)
+SEMAPHORES = (["vv", "tt", "ss", "lq", "lk0", "lk1", "lv", "out", "rx", "ry", "rc", "cyl", "ls"]
+              + ["qa%d" % r for r in range(4)] + ["am%d" % r for r in range(4)])
+
+SCALE = float(np.float32(0.0125))
+FLOOR = float(np.float32(np.exp(-20.0)))
+
+
+def rank_program(g, core, T, topo):
+    rank = T.rank_of(core)
+    if rank is None:
+        return
+    S = T.sem
+    cores = T.cores
+    n_ranks = len(cores)
+    Op, Fn, AX = AluOpType, ActivationFunctionType, AxisListType.X
+
+    def gate_of(c):
+        mine = [r for r in range(n_ranks) if topo.chip(cores[r]) == topo.chip(c)]
+        away = [r for r in range(n_ranks) if r not in mine]
+        ok = [r for r in mine if all(topo.may_write(cores[r], cores[a]) for a in away)]
+        return ok[0], [r for r in mine if r != ok[0]][0], away
+
+    def order_of(r):
+        ga, nb, away = gate_of(cores[r])
+        fg, fn, _ = gate_of(cores[away[0]])
+        return [r, nb if r == ga else ga, fg, fn]
+
+    gate, nbr, away = gate_of(core)
+    is_gate = rank == gate
+    order = order_of(rank)
+    _, PAR, FG, FN = order
+    lanes = topo.mask(core, cores[FG])
+    ne = bin(lanes).count("1")
+
+    queues = {"v": g.vector, "t": g.tensor, "s": g.scalar, "y": g.sync, "g": g}
+    tick = {"vv": 0, "tt": 0, "ss": 0}
+    seen = {}
+    total = {}
+
+    def wait(q, sem, n):
+        if n > 0 and seen.get((q, sem), 0) < n:
+            queues[q].wait_ge(S[sem] if False else T.sem[sem], n)
+            seen[(q, sem)] = n
+
+    def mark(ins, sem):
+        ins.then_inc(T.sem[sem], 1)
+        tick[sem] += 1
+        return tick[sem]
+
+    def V(ins):
+        return mark(ins, "vv")
+
+    def E(ins):
+        return mark(ins, "ss")
+
+    def M(ins):
+        return mark(ins, "tt")
+
+    sent = [0]
+
+    def send(src, dsts, sem):
+        ids = []
+        for r, _ in dsts:
+            rid, pid, _s = topo.addr(cores[r])
+            ids.append(DstId(rid=rid, pnc=pid))
+        g.remote_dma_fused([RemoteDMATransfer(dst_ids=ids, dma_engine_mask=lanes, remote_sem=T.sem[sem], srcs=[src],
+                                              dsts=[d for _, d in dsts])], local_sem=T.sem["ls"])
+        sent[0] += ne
+
+    def codes(slot):
+        return T.qc[:, 128 * slot:128 * slot + 128].bitcast(dt.uint8)
+
+    def scales(slot):
+        return T.qx[:, 128 * slot:128 * slot + 128]
+
+    def send_q(src_rank, to):
+        s = order.index(src_rank)
+        send(codes(s), [(r, codes(order_of(r).index(src_rank))) for r in to], "qa%d" % src_rank)
+        send(scales(s), [(r, scales(order_of(r).index(src_rank))) for r in to], "qa%d" % src_rank)
+
+    g.sync.dma_start(T.qt[:], T.q[:]).then_inc(S.lq, 16)
+    for h in range(2):
+        g.sync.dma_start(T.kt[:, 1024 * h:1024 * h + 1024], T.k[:, 1024 * h:1024 * h + 1024]).then_inc(T.sem["lk%d" % h], 16)
+    g.sync.dma_start(T.vt[:], T.v[:]).then_inc(S.lv, 16)
+
+    n_ot = V(g.vector.memset(T.ot[:], 1.0))
+    n_mask = V(g.vector.memset(T.mask[:], 1.0))
+    V(g.vector.memset(T.zr[:], 0.0))
+    V(g.vector.memset(T.cn[:, 16:32], 0.0))
+    wait("v", "lq", 16)
+    n_q = V(g.vector.quantize_mx(T.qc[:, 0:128], T.qx[:, 0:128], T.qt[:]))
+    wait("v", "vv", n_ot)
+    V(g.vector.quantize_mx(T.oc[:], T.ox[:], T.ot[:]))
+    wait("v", "vv", n_mask)
+    V(g.vector.memset(T.mask[:, 0:512:32], 0.0))
+    n_zero = V(g.vector.memset(T.zw[:], 0.0))
+
+    wait("g", "vv", n_q)
+    if is_gate:
+        send_q(rank, [FG, FN, PAR])
+        wait("g", "qa%d" % PAR, 2 * ne)
+        send_q(PAR, [FG, FN])
+    else:
+        send_q(rank, [PAR])
+
+    n_k = []
+    for h in range(2):
+        wait("v", "lk%d" % h, 16)
+        n_k.append(V(g.vector.quantize_mx(T.kc[:, 256 * h:256 * h + 256], T.kx[:, 256 * h:256 * h + 256],
+                                          T.kt[:, 1024 * h:1024 * h + 1024])))
+
+    n_S, n_neg, n_exp, n_cc, n_P, n_pq, n_L, n_A, n_lt, n_lc, n_ev = {}, {}, {}, {}, {}, {}, {}, {}, {}, {}, {}
+
+    def ps(k):
+        return T["ps%d" % (k % 2)]
+
+    def scores(k):
+        if k == 0:
+            wait("t", "vv", n_q)
+        else:
+            wait("t", "qa%d" % order[k], 2 * ne)
+        if k >= 2:
+            wait("t", "vv", n_lt[k - 2])
+            wait("t", "ss", n_ev[k - 2])
+        n_S[k] = []
+        for b in range(4):
+            wait("t", "vv", n_k[b // 2])
+            n_S[k].append(M(g.tensor.matmul_mx(ps(k)[:, 512 * b:512 * b + 128], T.kc[:, 128 * b:128 * b + 128],
+                                               T.kx[:, 128 * b:128 * b + 128], T.qc[:, 128 * k:128 * k + 128],
+                                               T.qx[:, 128 * k:128 * k + 128], True, True)))
+
+    def shift(k):
+        i = order[k]
+        t1 = T["t1_%d" % (k % 2)]
+        et = T["et%d" % (k % 2)]
+        for b in range(4):
+            wait("v", "tt", n_S[k][b])
+            n = V(g.vector.transpose(t1[:, b:512:4], ps(k)[:, 512 * b:512 * b + 128]))
+        wait("v", "vv", n)
+        lo, hi = 4 * k, 4 * k + 4
+        for b in range(4):
+            n = V(g.vector.tensor_reduce(T.r0[:, lo + b:lo + b + 1], t1[:, 128 * b:128 * b + 128], AX, Op.max, negate=True))
+        for src, dst, step in ((T.r0, T.r1, 64), (T.r1, T.r2, 32)):
+            wait("v", "vv", n)
+            for a in range(0, 128, step):
+                o = a ^ step
+                n = V(g.vector.tensor_tensor(dst[a:a + step, lo:hi], src[a:a + step, lo:hi], src[o:o + step, lo:hi], Op.min))
+        wait("v", "vv", n)
+        n_neg[k] = V(g.vector.tensor_scalar(T.cn[:, 4 * i:4 * i + 4], T.r2[:, lo:hi], SCALE, None, Op.mult))
+        wait("s", "vv", n_neg[k])
+        n_exp[k] = []
+        for b in range(4):
+            n_exp[k].append(E(g.scalar.activation(et[:, 128 * b:128 * b + 128], t1[:, 128 * b:128 * b + 128], Fn.Exp,
+                                                  bias=T.cn[:, 4 * i + b:4 * i + b + 1], scale=SCALE)))
+        if k in (1, 2):
+            n_cc[k] = E(g.scalar.activation(T["st%d" % k][:, 132:136], T.cn[:, 4 * i:4 * i + 4], Fn.Copy))
+        elif k == 3 and is_gate:
+            n_cc[k] = E(g.scalar.activation(T.cyb[:, 0:4], T.cn[:, 4 * i:4 * i + 4], Fn.Copy))
+
+    def pack(k):
+        et = T["et%d" % (k % 2)]
+        P = T["p%d" % k]
+        for b in range(4):
+            wait("v", "ss", n_exp[k][b])
+            n = V(g.vector.tensor_scalar(et[:, 128 * b:128 * b + 128], et[:, 128 * b:128 * b + 128], FLOOR, None, Op.max))
+        wait("v", "vv", n)
+        for b in range(4):
+            n = V(g.vector.transpose(P[:, b:512:4], et[:, b:512:4]))
+        wait("v", "vv", n)
+        n_P[k] = n
+        n_pq[k] = V(g.vector.quantize_mx(T.pc[:, 128 * k:128 * k + 128], T.px[:, 128 * k:128 * k + 128], P[:]))
+        wait("y", "vv", n)
+        g.sync.dma_start(T.p[order[k]], P[:]).then_inc(S.out, 16)
+        wait("t", "vv", max(n_pq[k], n_v[0]))
+        n_L[k] = M(g.tensor.matmul_mx(ps(k)[:, 512:640], T.oc[:], T.ox[:], T.pc[:, 128 * k:128 * k + 128],
+                                      T.px[:, 128 * k:128 * k + 128], True, True))
+        n_A[k] = M(g.tensor.matmul_mx(ps(k)[:, 0:128], T.vc[:], T.vx[:], T.pc[:, 128 * k:128 * k + 128],
+                                      T.px[:, 128 * k:128 * k + 128], True, True))
+        wait("s", "tt", n_A[k])
+        n_ev[k] = E(g.scalar.activation(T["st%d" % k][:, 0:128], ps(k)[:, 0:128], Fn.Copy))
+
+    def sums(k):
+        wait("v", "tt", n_L[k])
+        n_lt[k] = V(g.vector.transpose(T.lt[:, 128 * k:128 * k + 128], ps(k)[:, 512:640]))
+        wait("v", "vv", n_lt[k])
+        n_lc[k] = V(g.vector.tensor_copy(T["st%d" % k][:, 128:132], T.lt[:, 128 * k:128 * k + 128:32]))
+
+    n_v = [0]
+    scores(0)
+    shift(0)
+    wait("v", "lv", 16)
+    n_v[0] = V(g.vector.quantize_mx(T.vc[:], T.vx[:], T.vt[:]))
+    pack(0)
+    scores(1)
+    shift(1)
+    sums(0)
+    pack(1)
+    scores(2)
+    shift(2)
+    sums(1)
+    pack(2)
+    scores(3)
+    shift(3)
+    sums(2)
+    pack(3)
+    sums(3)
+
+    def ready(k):
+        wait("g", "vv", n_lc[k])
+        wait("g", "ss", n_ev[k])
+
+    def slot(r):
+        return lambda s: T["al%d" % order_of(r).index(s)]
+
+    ready(1)
+    send(T.st1[:], [(PAR, slot(PAR)(rank)[:])], "am%d" % rank)
+    if is_gate:
+        ready(2)
+        send(T.st2[:], [(FG, slot(FG)(rank)[:])], "am%d" % rank)
+        wait("g", "ss", n_cc[3])
+        wait("g", "rc", ne)
+        send(T.cyb[:], [(FN, T.cyl[:])], "cyl")
+        wait("g", "rx", ne)
+        send(T.fx[:], [(FG, slot(FG)(PAR)[:])], "am%d" % PAR)
+        ready(3)
+        send(T.st3[:, 0:132], [(FN, slot(FN)(rank)[:, 0:132])], "am%d" % rank)
+        wait("g", "ry", ne)
+        send(T.fy[:, 0:132], [(FN, slot(FN)(PAR)[:, 0:132])], "am%d" % PAR)
+    else:
+        wait("g", "vv", n_neg[3])
+        send(T.cn[:, 4 * FN:4 * FN + 4], [(PAR, T.cyb[:, 4:8])], "rc")
+        ready(2)
+        send(T.st2[:], [(PAR, T.fx[:])], "rx")
+        ready(3)
+        send(T.st3[:, 0:132], [(PAR, T.fy[:, 0:132])], "ry")
+
+    n = V(g.vector.transpose(T.ct[0:32, 0:32], T.cn[0:32, 0:32]))
+    wait("v", "vv", n)
+    n = V(g.vector.tensor_scalar(T.cu[0:32, :], T.ct[0:32, :], -1.0, None, Op.mult))
+    wait("y", "vv", n)
+    g.sync.dma_start(T.c[:], T.cu[0:16, :]).then_inc(S.out, 16)
+
+    def tiny(j):
+        return T.tiny[:, 4 * j:4 * j + 4]
+
+    wait("v", "am%d" % PAR, ne)
+    na = V(g.vector.tensor_tensor(tiny(0), T.cn[:, 4 * rank:4 * rank + 4], T.al1[:, 132:136], Op.min))
+    if is_gate:
+        wait("v", "am%d" % FG, ne)
+        wait("v", "am%d" % FN, ne)
+        neg = {FG: T.al2[:, 132:136], FN: T.al3[:, 132:136]}
+    else:
+        wait("v", "cyl", ne)
+        neg = {FG: T.cyl[:, 0:4], FN: T.cyl[:, 4:8]}
+    neg[rank] = T.cn[:, 4 * rank:4 * rank + 4]
+    neg[PAR] = T.al1[:, 132:136]
+    nb = V(g.vector.tensor_tensor(tiny(1), neg[FG], neg[FN], Op.min))
+    wait("v", "vv", nb)
+    n = V(g.vector.tensor_tensor(tiny(2), tiny(0), tiny(1), Op.min))
+    wait("v", "vv", n)
+    for j in order:
+        n = V(g.vector.tensor_tensor(T.dd[:, 4 * j:4 * j + 4], tiny(2), neg[j], Op.subtract))
+    wait("s", "vv", max(n, n_zero))
+    nx = E(g.scalar.activation(T.zw[:, 0:512:32], T.dd[:], Fn.Exp))
+    wait("v", "ss", nx)
+    n = V(g.vector.tensor_tensor_scan(T.wb[:], T.mask[:], T.zw[:], 0.0, Op.mult, Op.add))
+    wait("v", "vv", n)
+    n_w = V(g.vector.transpose(T.wr[:], T.wb[:]))
+    wait("y", "vv", n_w)
+    g.sync.dma_start(T.w[:], T.wr[0:1, :]).then_inc(S.out, 16)
+
+    def num(j):
+        return T.num[:, 128 * j:128 * j + 128]
+
+    src = {rank: T.st0, PAR: T.al1, FG: T.al2, FN: T.al3}
+    den = acc = None
+    for j, r in enumerate(order):
+        if j == 0:
+            wait("v", "ss", n_ev[0])
+        else:
+            wait("v", "am%d" % r, ne)
+        nd = V(g.vector.tensor_tensor(tiny(4 + 2 * j), src[r][:, 128:132], T.zw[:, 128 * r:128 * r + 128:32], Op.mult))
+        wait("v", "vv", n_w)
+        nn = V(g.vector.tensor_tensor(num(2 * j), src[r][:, 0:128], T.wr[:, 128 * r:128 * r + 128], Op.mult))
+        if j:
+            wait("v", "vv", nd)
+            nd = V(g.vector.tensor_tensor(tiny(5 + 2 * j), den, tiny(4 + 2 * j), Op.add))
+            den = tiny(5 + 2 * j)
+            wait("v", "vv", nn)
+            nn = V(g.vector.tensor_tensor(num(2 * j + 1), acc, num(2 * j), Op.add))
+            acc = num(2 * j + 1)
+        else:
+            den, acc = tiny(4), num(0)
+        if j == len(order) - 1:
+            wait("v", "vv", nd)
+            nr = V(g.vector.reciprocal(T.zr[:, 0:128:32], den))
+            wait("v", "vv", nr)
+            nr = V(g.vector.tensor_tensor_scan(T.rb[:], T.mask[:, 0:128], T.zr[:], 0.0, Op.mult, Op.add))
+            wait("v", "vv", nr)
+            nr = V(g.vector.transpose(T.rw[:], T.rb[:]))
+            wait("v", "vv", nr)
+            nr = V(g.vector.tensor_tensor(T.res[:], acc, T.rw[:], Op.mult))
+    wait("y", "vv", nr)
+    g.sync.dma_start(T.o[:], T.res[:]).then_inc(S.out, 16)
+    g.sync.wait_ge(S.out, 16 * 7)
+    wait("g", "ss", tick["ss"])
+    wait("g", "tt", tick["tt"])
+    wait("g", "ls", sent[0])

@@ -18,7 +18,8 @@ SCRATCH = {
     "r0": ("sbuf", [128, 16], F), "r1": ("sbuf", [128, 16], F), "r2": ("sbuf", [128, 16], F),
     "lt": ("sbuf", [128, 512], F),
     "fx": ("sbuf", [128, 136], F), "fy": ("sbuf", [128, 136], F),
-    "cyb": ("sbuf", [128, 8], F), "cyl": ("sbuf", [128, 8], F),
+    "cyb": ("sbuf", [128, 12], F), "cyl": ("sbuf", [128, 8], F), "cys": ("sbuf", [128, 8], F),
+    "cpl": ("sbuf", [128, 4], F),
     "mask": ("sbuf", [128, 512], F), "zw": ("sbuf", [128, 512], F), "wb": ("sbuf", [128, 512], F),
     "wr": ("sbuf", [128, 512], F), "zr": ("sbuf", [128, 128], F), "rb": ("sbuf", [128, 128], F),
     "rw": ("sbuf", [128, 128], F), "dd": ("sbuf", [128, 16], F), "tiny": ("sbuf", [128, 64], F),
@@ -28,13 +29,12 @@ SCRATCH = {
 for _k in range(4):
     SCRATCH["p%d" % _k] = ("sbuf", [128, 512], B)
     SCRATCH["st%d" % _k] = ("sbuf", [128, 136], F)
-    if _k < 2:
-        SCRATCH["t1_%d" % _k] = ("sbuf", [128, 512], F)
-        SCRATCH["et%d" % _k] = ("sbuf", [128, 512], B)
+    SCRATCH["t1_%d" % _k] = ("sbuf", [128, 512], F)
+    SCRATCH["et%d" % _k] = ("sbuf", [128, 512], B)
     if _k:
         SCRATCH["al%d" % _k] = ("sbuf", [128, 136], F)
-SEMAPHORES = (["vv", "tt", "ss", "lq", "lk0", "lk1", "lv", "out", "rx", "ry", "rc", "cyl", "ls"]
-              + ["qa%d" % r for r in range(4)] + ["am%d" % r for r in range(4)])
+SEMAPHORES = (["vv", "tt", "ss", "lq", "lv", "out", "rx", "ry", "rc", "cp", "cyl", "ls"]
+              + ["lk%d" % r for r in range(4)] + ["qa%d" % r for r in range(4)] + ["am%d" % r for r in range(4)])
 
 SCALE = float(np.float32(0.0125))
 FLOOR = float(np.float32(np.exp(-20.0)))
@@ -64,17 +64,17 @@ def rank_program(g, core, T, topo):
     is_gate = rank == gate
     order = order_of(rank)
     _, PAR, FG, FN = order
+    OWN_, PAR_, X_, Y_ = 0, 1, 2, 3
     lanes = topo.mask(core, cores[FG])
     ne = bin(lanes).count("1")
 
     queues = {"v": g.vector, "t": g.tensor, "s": g.scalar, "y": g.sync, "g": g}
     tick = {"vv": 0, "tt": 0, "ss": 0}
     seen = {}
-    total = {}
 
     def wait(q, sem, n):
         if n > 0 and seen.get((q, sem), 0) < n:
-            queues[q].wait_ge(S[sem] if False else T.sem[sem], n)
+            queues[q].wait_ge(T.sem[sem], n)
             seen[(q, sem)] = n
 
     def mark(ins, sem):
@@ -114,8 +114,8 @@ def rank_program(g, core, T, topo):
         send(scales(s), [(r, scales(order_of(r).index(src_rank))) for r in to], "qa%d" % src_rank)
 
     g.sync.dma_start(T.qt[:], T.q[:]).then_inc(S.lq, 16)
-    for h in range(2):
-        g.sync.dma_start(T.kt[:, 1024 * h:1024 * h + 1024], T.k[:, 1024 * h:1024 * h + 1024]).then_inc(T.sem["lk%d" % h], 16)
+    for h in range(4):
+        g.sync.dma_start(T.kt[:, 512 * h:512 * h + 512], T.k[:, 512 * h:512 * h + 512]).then_inc(T.sem["lk%d" % h], 16)
     g.sync.dma_start(T.vt[:], T.v[:]).then_inc(S.lv, 16)
 
     n_ot = V(g.vector.memset(T.ot[:], 1.0))
@@ -139,38 +139,39 @@ def rank_program(g, core, T, topo):
         send_q(rank, [PAR])
 
     n_k = []
-    for h in range(2):
+    for h in range(4):
         wait("v", "lk%d" % h, 16)
-        n_k.append(V(g.vector.quantize_mx(T.kc[:, 256 * h:256 * h + 256], T.kx[:, 256 * h:256 * h + 256],
-                                          T.kt[:, 1024 * h:1024 * h + 1024])))
+        n_k.append(V(g.vector.quantize_mx(T.kc[:, 128 * h:128 * h + 128], T.kx[:, 128 * h:128 * h + 128],
+                                          T.kt[:, 512 * h:512 * h + 512])))
 
-    n_S, n_neg, n_exp, n_cc, n_P, n_pq, n_L, n_A, n_lt, n_lc, n_ev = {}, {}, {}, {}, {}, {}, {}, {}, {}, {}, {}
+    n_S, n_T, n_neg, n_exp, n_cc, n_P, n_pq, n_L, n_A, n_lt, n_lc, n_ev = {}, {}, {}, {}, {}, {}, {}, {}, {}, {}, {}, {}
+    PSET = {X_: T.ps0, PAR_: T.ps1, Y_: T.ps1, OWN_: T.ps0}
+    BANK = {X_: 0, PAR_: 2, Y_: 0, OWN_: 0}
 
-    def ps(k):
-        return T["ps%d" % (k % 2)]
-
-    def scores(k):
-        if k == 0:
+    def scores(k, free=()):
+        if k == OWN_:
             wait("t", "vv", n_q)
         else:
             wait("t", "qa%d" % order[k], 2 * ne)
-        if k >= 2:
-            wait("t", "vv", n_lt[k - 2])
-            wait("t", "ss", n_ev[k - 2])
+        for sem, n in free:
+            wait("t", sem, n)
         n_S[k] = []
         for b in range(4):
-            wait("t", "vv", n_k[b // 2])
-            n_S[k].append(M(g.tensor.matmul_mx(ps(k)[:, 512 * b:512 * b + 128], T.kc[:, 128 * b:128 * b + 128],
+            wait("t", "vv", n_k[b])
+            n_S[k].append(M(g.tensor.matmul_mx(PSET[k][:, 512 * b:512 * b + 128], T.kc[:, 128 * b:128 * b + 128],
                                                T.kx[:, 128 * b:128 * b + 128], T.qc[:, 128 * k:128 * k + 128],
                                                T.qx[:, 128 * k:128 * k + 128], True, True)))
 
+    def cneg(k):
+        return T.cn[:, 4 * order[k]:4 * order[k] + 4]
+
     def shift(k):
-        i = order[k]
-        t1 = T["t1_%d" % (k % 2)]
-        et = T["et%d" % (k % 2)]
+        t1 = T["t1_%d" % k]
+        et = T["et%d" % k]
         for b in range(4):
             wait("v", "tt", n_S[k][b])
-            n = V(g.vector.transpose(t1[:, b:512:4], ps(k)[:, 512 * b:512 * b + 128]))
+            n = V(g.vector.transpose(t1[:, b:512:4], PSET[k][:, 512 * b:512 * b + 128]))
+        n_T[k] = n
         wait("v", "vv", n)
         lo, hi = 4 * k, 4 * k + 4
         for b in range(4):
@@ -181,116 +182,127 @@ def rank_program(g, core, T, topo):
                 o = a ^ step
                 n = V(g.vector.tensor_tensor(dst[a:a + step, lo:hi], src[a:a + step, lo:hi], src[o:o + step, lo:hi], Op.min))
         wait("v", "vv", n)
-        n_neg[k] = V(g.vector.tensor_scalar(T.cn[:, 4 * i:4 * i + 4], T.r2[:, lo:hi], SCALE, None, Op.mult))
+        n_neg[k] = V(g.vector.tensor_scalar(cneg(k), T.r2[:, lo:hi], SCALE, None, Op.mult))
         wait("s", "vv", n_neg[k])
         n_exp[k] = []
         for b in range(4):
             n_exp[k].append(E(g.scalar.activation(et[:, 128 * b:128 * b + 128], t1[:, 128 * b:128 * b + 128], Fn.Exp,
-                                                  bias=T.cn[:, 4 * i + b:4 * i + b + 1], scale=SCALE)))
-        if k in (1, 2):
-            n_cc[k] = E(g.scalar.activation(T["st%d" % k][:, 132:136], T.cn[:, 4 * i:4 * i + 4], Fn.Copy))
-        elif k == 3 and is_gate:
-            n_cc[k] = E(g.scalar.activation(T.cyb[:, 0:4], T.cn[:, 4 * i:4 * i + 4], Fn.Copy))
+                                                  bias=cneg(k)[:, b:b + 1] if False else
+                                                  T.cn[:, 4 * order[k] + b:4 * order[k] + b + 1], scale=SCALE)))
+        to = {X_: T.st2[:, 132:136], Y_: T.cyb[:, 0:4] if is_gate else T.cys[:, 0:4],
+              PAR_: None if is_gate else T.cys[:, 4:8], OWN_: None}[k]
+        if to is not None:
+            n_cc[k] = E(g.scalar.activation(to, cneg(k), Fn.Copy))
 
-    def pack(k):
-        et = T["et%d" % (k % 2)]
-        P = T["p%d" % k]
+    def clamp(k):
+        et = T["et%d" % k]
         for b in range(4):
             wait("v", "ss", n_exp[k][b])
-            n = V(g.vector.tensor_scalar(et[:, 128 * b:128 * b + 128], et[:, 128 * b:128 * b + 128], FLOOR, None, Op.max))
-        wait("v", "vv", n)
+            n_P[k] = V(g.vector.tensor_scalar(et[:, 128 * b:128 * b + 128], et[:, 128 * b:128 * b + 128], FLOOR, None, Op.max))
+
+    def pack(k):
+        et = T["et%d" % k]
+        P = T["p%d" % k]
+        wait("v", "vv", n_P[k])
         for b in range(4):
             n = V(g.vector.transpose(P[:, b:512:4], et[:, b:512:4]))
         wait("v", "vv", n)
-        n_P[k] = n
         n_pq[k] = V(g.vector.quantize_mx(T.pc[:, 128 * k:128 * k + 128], T.px[:, 128 * k:128 * k + 128], P[:]))
         wait("y", "vv", n)
         g.sync.dma_start(T.p[order[k]], P[:]).then_inc(S.out, 16)
-        wait("t", "vv", max(n_pq[k], n_v[0]))
-        n_L[k] = M(g.tensor.matmul_mx(ps(k)[:, 512:640], T.oc[:], T.ox[:], T.pc[:, 128 * k:128 * k + 128],
+        wait("t", "vv", n_pq[k])
+        c = 512 * BANK[k]
+        n_L[k] = M(g.tensor.matmul_mx(PSET[k][:, c + 512:c + 640], T.oc[:], T.ox[:], T.pc[:, 128 * k:128 * k + 128],
                                       T.px[:, 128 * k:128 * k + 128], True, True))
-        n_A[k] = M(g.tensor.matmul_mx(ps(k)[:, 0:128], T.vc[:], T.vx[:], T.pc[:, 128 * k:128 * k + 128],
+        n_A[k] = M(g.tensor.matmul_mx(PSET[k][:, c:c + 128], T.vc[:], T.vx[:], T.pc[:, 128 * k:128 * k + 128],
                                       T.px[:, 128 * k:128 * k + 128], True, True))
         wait("s", "tt", n_A[k])
-        n_ev[k] = E(g.scalar.activation(T["st%d" % k][:, 0:128], ps(k)[:, 0:128], Fn.Copy))
+        n_ev[k] = E(g.scalar.activation(T["st%d" % k][:, 0:128], PSET[k][:, c:c + 128], Fn.Copy))
 
     def sums(k):
+        c = 512 * BANK[k] + 512
         wait("v", "tt", n_L[k])
-        n_lt[k] = V(g.vector.transpose(T.lt[:, 128 * k:128 * k + 128], ps(k)[:, 512:640]))
+        n_lt[k] = V(g.vector.transpose(T.lt[:, 128 * k:128 * k + 128], PSET[k][:, c:c + 128]))
         wait("v", "vv", n_lt[k])
         n_lc[k] = V(g.vector.tensor_copy(T["st%d" % k][:, 128:132], T.lt[:, 128 * k:128 * k + 128:32]))
 
-    n_v = [0]
-    scores(0)
-    shift(0)
+    scores(X_)
+    shift(X_)
     wait("v", "lv", 16)
-    n_v[0] = V(g.vector.quantize_mx(T.vc[:], T.vx[:], T.vt[:]))
-    pack(0)
-    scores(1)
-    shift(1)
-    sums(0)
-    pack(1)
-    scores(2)
-    shift(2)
-    sums(1)
-    pack(2)
-    scores(3)
-    shift(3)
-    sums(2)
-    pack(3)
-    sums(3)
+    V(g.vector.quantize_mx(T.vc[:], T.vx[:], T.vt[:]))
+    scores(PAR_)
+    shift(PAR_)
+    clamp(X_)
+    scores(Y_, [("vv", n_T[PAR_])])
+    pack(X_)
+    shift(Y_)
+    sums(X_)
+    clamp(Y_)
+    pack(Y_)
+    scores(OWN_, [("vv", n_lt[X_]), ("ss", n_ev[X_])])
+    clamp(PAR_)
+    sums(Y_)
+    pack(PAR_)
+    shift(OWN_)
+    sums(PAR_)
+    clamp(OWN_)
+    pack(OWN_)
 
     def ready(k):
         wait("g", "vv", n_lc[k])
         wait("g", "ss", n_ev[k])
 
-    def slot(r):
-        return lambda s: T["al%d" % order_of(r).index(s)]
+    def land(r, s):
+        return T["al%d" % order_of(r).index(s)]
 
-    ready(1)
-    send(T.st1[:], [(PAR, slot(PAR)(rank)[:])], "am%d" % rank)
     if is_gate:
-        ready(2)
-        send(T.st2[:], [(FG, slot(FG)(rank)[:])], "am%d" % rank)
-        wait("g", "ss", n_cc[3])
+        wait("g", "vv", n_neg[PAR_])
+        send(cneg(PAR_), [(PAR, T.cpl[:])], "cp")
+        ready(X_)
+        wait("g", "ss", n_cc[X_])
+        send(T.st2[:], [(FG, land(FG, rank)[:])], "am%d" % rank)
+        wait("g", "ss", n_cc[Y_])
         wait("g", "rc", ne)
-        send(T.cyb[:], [(FN, T.cyl[:])], "cyl")
+        send(T.cyb[:, 0:8], [(FN, T.cyl[:])], "cyl")
         wait("g", "rx", ne)
-        send(T.fx[:], [(FG, slot(FG)(PAR)[:])], "am%d" % PAR)
-        ready(3)
-        send(T.st3[:, 0:132], [(FN, slot(FN)(rank)[:, 0:132])], "am%d" % rank)
+        send(T.fx[:], [(FG, land(FG, PAR)[:])], "am%d" % PAR)
+        ready(Y_)
+        send(T.st3[:, 0:132], [(FN, land(FN, rank)[:, 0:132])], "am%d" % rank)
         wait("g", "ry", ne)
-        send(T.fy[:, 0:132], [(FN, slot(FN)(PAR)[:, 0:132])], "am%d" % PAR)
+        send(T.fy[:, 0:132], [(FN, land(FN, PAR)[:, 0:132])], "am%d" % PAR)
     else:
-        wait("g", "vv", n_neg[3])
-        send(T.cn[:, 4 * FN:4 * FN + 4], [(PAR, T.cyb[:, 4:8])], "rc")
-        ready(2)
+        wait("g", "ss", n_cc[Y_])
+        send(T.cys[:], [(PAR, T.cyb[:, 4:12])], "rc")
+        ready(X_)
         send(T.st2[:], [(PAR, T.fx[:])], "rx")
-        ready(3)
+        ready(Y_)
         send(T.st3[:, 0:132], [(PAR, T.fy[:, 0:132])], "ry")
+    ready(PAR_)
+    send(T.st1[:, 0:132], [(PAR, land(PAR, rank)[:, 0:132])], "am%d" % rank)
 
     n = V(g.vector.transpose(T.ct[0:32, 0:32], T.cn[0:32, 0:32]))
     wait("v", "vv", n)
     n = V(g.vector.tensor_scalar(T.cu[0:32, :], T.ct[0:32, :], -1.0, None, Op.mult))
     wait("y", "vv", n)
     g.sync.dma_start(T.c[:], T.cu[0:16, :]).then_inc(S.out, 16)
+    sums(OWN_)
 
     def tiny(j):
         return T.tiny[:, 4 * j:4 * j + 4]
 
-    wait("v", "am%d" % PAR, ne)
-    na = V(g.vector.tensor_tensor(tiny(0), T.cn[:, 4 * rank:4 * rank + 4], T.al1[:, 132:136], Op.min))
     if is_gate:
+        wait("v", "rc", ne)
         wait("v", "am%d" % FG, ne)
         wait("v", "am%d" % FN, ne)
-        neg = {FG: T.al2[:, 132:136], FN: T.al3[:, 132:136]}
+        neg = {PAR: T.cyb[:, 8:12], FG: T.al2[:, 132:136], FN: T.al3[:, 132:136]}
     else:
+        wait("v", "cp", ne)
         wait("v", "cyl", ne)
-        neg = {FG: T.cyl[:, 0:4], FN: T.cyl[:, 4:8]}
-    neg[rank] = T.cn[:, 4 * rank:4 * rank + 4]
-    neg[PAR] = T.al1[:, 132:136]
-    nb = V(g.vector.tensor_tensor(tiny(1), neg[FG], neg[FN], Op.min))
-    wait("v", "vv", nb)
+        neg = {PAR: T.cpl[:], FG: T.cyl[:, 0:4], FN: T.cyl[:, 4:8]}
+    neg[rank] = cneg(OWN_)
+    V(g.vector.tensor_tensor(tiny(0), neg[rank], neg[PAR], Op.min))
+    n = V(g.vector.tensor_tensor(tiny(1), neg[FG], neg[FN], Op.min))
+    wait("v", "vv", n)
     n = V(g.vector.tensor_tensor(tiny(2), tiny(0), tiny(1), Op.min))
     wait("v", "vv", n)
     for j in order:
@@ -309,13 +321,14 @@ def rank_program(g, core, T, topo):
 
     src = {rank: T.st0, PAR: T.al1, FG: T.al2, FN: T.al3}
     den = acc = None
-    for j, r in enumerate(order):
-        if j == 0:
-            wait("v", "ss", n_ev[0])
+    arrive = [FG, FN, rank, PAR] if is_gate else [rank, FG, PAR, FN]
+    for j, r in enumerate(arrive):
+        if r == rank:
+            wait("v", "ss", n_ev[OWN_])
         else:
             wait("v", "am%d" % r, ne)
         nd = V(g.vector.tensor_tensor(tiny(4 + 2 * j), src[r][:, 128:132], T.zw[:, 128 * r:128 * r + 128:32], Op.mult))
-        wait("v", "vv", n_w)
+        wait("v", "vv", max(n_w, n_lc[OWN_]))
         nn = V(g.vector.tensor_tensor(num(2 * j), src[r][:, 0:128], T.wr[:, 128 * r:128 * r + 128], Op.mult))
         if j:
             wait("v", "vv", nd)
@@ -326,15 +339,14 @@ def rank_program(g, core, T, topo):
             acc = num(2 * j + 1)
         else:
             den, acc = tiny(4), num(0)
-        if j == len(order) - 1:
-            wait("v", "vv", nd)
-            nr = V(g.vector.reciprocal(T.zr[:, 0:128:32], den))
-            wait("v", "vv", nr)
-            nr = V(g.vector.tensor_tensor_scan(T.rb[:], T.mask[:, 0:128], T.zr[:], 0.0, Op.mult, Op.add))
-            wait("v", "vv", nr)
-            nr = V(g.vector.transpose(T.rw[:], T.rb[:]))
-            wait("v", "vv", nr)
-            nr = V(g.vector.tensor_tensor(T.res[:], acc, T.rw[:], Op.mult))
+    wait("v", "vv", nd)
+    nr = V(g.vector.reciprocal(T.zr[:, 0:128:32], den))
+    wait("v", "vv", nr)
+    nr = V(g.vector.tensor_tensor_scan(T.rb[:], T.mask[:, 0:128], T.zr[:], 0.0, Op.mult, Op.add))
+    wait("v", "vv", nr)
+    nr = V(g.vector.transpose(T.rw[:], T.rb[:]))
+    wait("v", "vv", nr)
+    nr = V(g.vector.tensor_tensor(T.res[:], acc, T.rw[:], Op.mult))
     wait("y", "vv", nr)
     g.sync.dma_start(T.o[:], T.res[:]).then_inc(S.out, 16)
     g.sync.wait_ge(S.out, 16 * 7)

@@ -14,12 +14,12 @@ SCRATCH = {
     "vc": ("sbuf", [128, 128], C4), "vx": ("sbuf", [128, 128], U8),
     "oc": ("sbuf", [128, 128], C4), "ox": ("sbuf", [128, 128], U8),
     "pc": ("sbuf", [128, 512], C4), "px": ("sbuf", [128, 512], U8),
-    "cn": ("sbuf", [128, 32], F), "ct": ("sbuf", [128, 32], F), "cu": ("sbuf", [128, 32], F),
+    "cn": ("sbuf", [128, 32], F),
+    "ct": ("sbuf", [128, 32], F), "cu": ("sbuf", [128, 32], F),
     "r0": ("sbuf", [128, 16], F), "r1": ("sbuf", [128, 16], F), "r2": ("sbuf", [128, 16], F),
     "lt": ("sbuf", [128, 512], F),
-    "fx": ("sbuf", [128, 136], F), "fy": ("sbuf", [128, 136], F),
-    "cyb": ("sbuf", [128, 12], F), "cyl": ("sbuf", [128, 8], F), "cys": ("sbuf", [128, 8], F),
-    "cpl": ("sbuf", [128, 4], F),
+    "fx": ("sbuf", [128, 132], F), "fy": ("sbuf", [128, 132], F), "fc": ("sbuf", [128, 8], F),
+    "cyl": ("sbuf", [128, 16], F), "cpl": ("sbuf", [128, 4], F),
     "mask": ("sbuf", [128, 512], F), "zw": ("sbuf", [128, 512], F), "wb": ("sbuf", [128, 512], F),
     "wr": ("sbuf", [128, 512], F), "zr": ("sbuf", [128, 128], F), "rb": ("sbuf", [128, 128], F),
     "rw": ("sbuf", [128, 128], F), "dd": ("sbuf", [128, 16], F), "tiny": ("sbuf", [128, 64], F),
@@ -28,16 +28,28 @@ SCRATCH = {
 }
 for _k in range(4):
     SCRATCH["p%d" % _k] = ("sbuf", [128, 512], B)
-    SCRATCH["st%d" % _k] = ("sbuf", [128, 136], F)
+    SCRATCH["st%d" % _k] = ("sbuf", [128, 132], F)
     SCRATCH["t1_%d" % _k] = ("sbuf", [128, 512], F)
     SCRATCH["et%d" % _k] = ("sbuf", [128, 512], B)
     if _k:
-        SCRATCH["al%d" % _k] = ("sbuf", [128, 136], F)
+        SCRATCH["al%d" % _k] = ("sbuf", [128, 132], F)
 SEMAPHORES = (["vv", "tt", "ss", "lq", "lv", "out", "rx", "ry", "rc", "cp", "cyl", "ls"]
               + ["lk%d" % r for r in range(4)] + ["qa%d" % r for r in range(4)] + ["am%d" % r for r in range(4)])
 
 SCALE = float(np.float32(0.0125))
 FLOOR = float(np.float32(np.exp(-20.0)))
+
+PLAN_GATE = {
+    "steps": "S0 h0 v S1 h1 c1 S2 p1 h2 u1 c2 S3 p2 h3 u2 c3 p3 c0 u3 p0 u0 C",
+    "sets": {0: 0, 1: 1, 2: 0, 3: 1}, "al": {0: (0, 2), 1: (1, 0), 2: (0, 0), 3: (1, 0)},
+    "sends": ["c neighbour", "A neighbour", "c far", "A far gate", "pass c", "pass far gate", "A far neighbour",
+              "pass far neighbour"],
+}
+PLAN_NEIGHBOUR = {
+    "steps": "S0 h0 S2 h2 v c2 S3 p2 h3 u2 c3 p3 S1 c0 u3 h1 c1 p1 p0 u1 u0 C",
+    "sets": {0: 1, 1: 0, 2: 0, 3: 1}, "al": {0: (1, 2), 1: (0, 0), 2: (0, 0), 3: (1, 0)},
+    "sends": ["c far", "A far gate", "A far neighbour", "c neighbour", "A neighbour"],
+}
 
 
 def rank_program(g, core, T, topo):
@@ -62,6 +74,7 @@ def rank_program(g, core, T, topo):
 
     gate, nbr, away = gate_of(core)
     is_gate = rank == gate
+    plan = PLAN_GATE if is_gate else PLAN_NEIGHBOUR
     order = order_of(rank)
     _, PAR, FG, FN = order
     OWN_, PAR_, X_, Y_ = 0, 1, 2, 3
@@ -108,10 +121,17 @@ def rank_program(g, core, T, topo):
     def scales(slot):
         return T.qx[:, 128 * slot:128 * slot + 128]
 
-    def send_q(src_rank, to):
-        s = order.index(src_rank)
-        send(codes(s), [(r, codes(order_of(r).index(src_rank))) for r in to], "qa%d" % src_rank)
-        send(scales(s), [(r, scales(order_of(r).index(src_rank))) for r in to], "qa%d" % src_rank)
+    def slot_at(r, s):
+        return order_of(r).index(s)
+
+    def land(r, s):
+        return T["al%d" % slot_at(r, s)][:]
+
+    def send_q(s, to):
+        k = slot_at(rank, s)
+        for r in to:
+            send(codes(k), [(r, codes(slot_at(r, s)))], "qa%d" % s)
+            send(scales(k), [(r, scales(slot_at(r, s)))], "qa%d" % s)
 
     g.sync.dma_start(T.qt[:], T.q[:]).then_inc(S.lq, 16)
     for h in range(4):
@@ -132,11 +152,10 @@ def rank_program(g, core, T, topo):
 
     wait("g", "vv", n_q)
     if is_gate:
-        send_q(rank, [FG, FN, PAR])
+        send_q(rank, [FN, FG])
         wait("g", "qa%d" % PAR, 2 * ne)
-        send_q(PAR, [FG, FN])
-    else:
-        send_q(rank, [PAR])
+        send_q(PAR, [FN, FG])
+    send_q(rank, [PAR])
 
     n_k = []
     for h in range(4):
@@ -144,23 +163,37 @@ def rank_program(g, core, T, topo):
         n_k.append(V(g.vector.quantize_mx(T.kc[:, 128 * h:128 * h + 128], T.kx[:, 128 * h:128 * h + 128],
                                           T.kt[:, 512 * h:512 * h + 512])))
 
-    n_S, n_T, n_neg, n_exp, n_cc, n_P, n_pq, n_L, n_A, n_lt, n_lc, n_ev = {}, {}, {}, {}, {}, {}, {}, {}, {}, {}, {}, {}
-    PSET = {X_: T.ps0, PAR_: T.ps1, Y_: T.ps1, OWN_: T.ps0}
-    BANK = {X_: 0, PAR_: 2, Y_: 0, OWN_: 0}
+    n_S, n_T, n_neg, n_exp, n_P, n_pq, n_L, n_A, n_lt, n_lc, n_ev = {}, {}, {}, {}, {}, {}, {}, {}, {}, {}, {}
+    psum = [T.ps0, T.ps1]
+    holds = {}
 
-    def scores(k, free=()):
+    def bank(at, taker):
+        if at in holds:
+            wait("t", *holds[at]())
+        holds[at] = taker
+        return psum[at[0]][:, 512 * at[1]:512 * at[1] + 128]
+
+    def where(k, j):
+        s, b = plan["al"][k]
+        return s, b + j
+
+    def view(at):
+        return psum[at[0]][:, 512 * at[1]:512 * at[1] + 128]
+
+    def words(buf, k):
+        return buf[:, 128 * k:128 * k + 128]
+
+    def scores(k):
         if k == OWN_:
             wait("t", "vv", n_q)
         else:
             wait("t", "qa%d" % order[k], 2 * ne)
-        for sem, n in free:
-            wait("t", sem, n)
         n_S[k] = []
         for b in range(4):
+            out = bank((plan["sets"][k], b), lambda k=k, b=b: ("vv", n_T[k][b]))
             wait("t", "vv", n_k[b])
-            n_S[k].append(M(g.tensor.matmul_mx(PSET[k][:, 512 * b:512 * b + 128], T.kc[:, 128 * b:128 * b + 128],
-                                               T.kx[:, 128 * b:128 * b + 128], T.qc[:, 128 * k:128 * k + 128],
-                                               T.qx[:, 128 * k:128 * k + 128], True, True)))
+            n_S[k].append(M(g.tensor.matmul_mx(out, words(T.kc, b), words(T.kx, b), words(T.qc, k), words(T.qx, k),
+                                               True, True)))
 
     def cneg(k):
         return T.cn[:, 4 * order[k]:4 * order[k] + 4]
@@ -168,11 +201,11 @@ def rank_program(g, core, T, topo):
     def shift(k):
         t1 = T["t1_%d" % k]
         et = T["et%d" % k]
+        n_T[k] = []
         for b in range(4):
             wait("v", "tt", n_S[k][b])
-            n = V(g.vector.transpose(t1[:, b:512:4], PSET[k][:, 512 * b:512 * b + 128]))
-        n_T[k] = n
-        wait("v", "vv", n)
+            n_T[k].append(V(g.vector.transpose(t1[:, b:512:4], view((plan["sets"][k], b)))))
+        wait("v", "vv", n_T[k][3])
         lo, hi = 4 * k, 4 * k + 4
         for b in range(4):
             n = V(g.vector.tensor_reduce(T.r0[:, lo + b:lo + b + 1], t1[:, 128 * b:128 * b + 128], AX, Op.max, negate=True))
@@ -185,14 +218,10 @@ def rank_program(g, core, T, topo):
         n_neg[k] = V(g.vector.tensor_scalar(cneg(k), T.r2[:, lo:hi], SCALE, None, Op.mult))
         wait("s", "vv", n_neg[k])
         n_exp[k] = []
+        c = 4 * order[k]
         for b in range(4):
             n_exp[k].append(E(g.scalar.activation(et[:, 128 * b:128 * b + 128], t1[:, 128 * b:128 * b + 128], Fn.Exp,
-                                                  bias=cneg(k)[:, b:b + 1] if False else
-                                                  T.cn[:, 4 * order[k] + b:4 * order[k] + b + 1], scale=SCALE)))
-        to = {X_: T.st2[:, 132:136], Y_: T.cyb[:, 0:4] if is_gate else T.cys[:, 0:4],
-              PAR_: None if is_gate else T.cys[:, 4:8], OWN_: None}[k]
-        if to is not None:
-            n_cc[k] = E(g.scalar.activation(to, cneg(k), Fn.Copy))
+                                                  bias=T.cn[:, c + b:c + b + 1], scale=SCALE)))
 
     def clamp(k):
         et = T["et%d" % k]
@@ -207,99 +236,79 @@ def rank_program(g, core, T, topo):
         for b in range(4):
             n = V(g.vector.transpose(P[:, b:512:4], et[:, b:512:4]))
         wait("v", "vv", n)
-        n_pq[k] = V(g.vector.quantize_mx(T.pc[:, 128 * k:128 * k + 128], T.px[:, 128 * k:128 * k + 128], P[:]))
+        n_pq[k] = V(g.vector.quantize_mx(words(T.pc, k), words(T.px, k), P[:]))
         wait("y", "vv", n)
         g.sync.dma_start(T.p[order[k]], P[:]).then_inc(S.out, 16)
         wait("t", "vv", n_pq[k])
-        c = 512 * BANK[k]
-        n_L[k] = M(g.tensor.matmul_mx(PSET[k][:, c + 512:c + 640], T.oc[:], T.ox[:], T.pc[:, 128 * k:128 * k + 128],
-                                      T.px[:, 128 * k:128 * k + 128], True, True))
-        n_A[k] = M(g.tensor.matmul_mx(PSET[k][:, c:c + 128], T.vc[:], T.vx[:], T.pc[:, 128 * k:128 * k + 128],
-                                      T.px[:, 128 * k:128 * k + 128], True, True))
+        out = bank(where(k, 1), lambda k=k: ("vv", n_lt[k]))
+        n_L[k] = M(g.tensor.matmul_mx(out, T.oc[:], T.ox[:], words(T.pc, k), words(T.px, k), True, True))
+        out = bank(where(k, 0), lambda k=k: ("ss", n_ev[k]))
+        n_A[k] = M(g.tensor.matmul_mx(out, T.vc[:], T.vx[:], words(T.pc, k), words(T.px, k), True, True))
         wait("s", "tt", n_A[k])
-        n_ev[k] = E(g.scalar.activation(T["st%d" % k][:, 0:128], PSET[k][:, c:c + 128], Fn.Copy))
+        n_ev[k] = E(g.scalar.activation(T["st%d" % k][:, 0:128], view(where(k, 0)), Fn.Copy))
 
     def sums(k):
-        c = 512 * BANK[k] + 512
         wait("v", "tt", n_L[k])
-        n_lt[k] = V(g.vector.transpose(T.lt[:, 128 * k:128 * k + 128], PSET[k][:, c:c + 128]))
+        n_lt[k] = V(g.vector.transpose(words(T.lt, k), view(where(k, 1))))
         wait("v", "vv", n_lt[k])
         n_lc[k] = V(g.vector.tensor_copy(T["st%d" % k][:, 128:132], T.lt[:, 128 * k:128 * k + 128:32]))
 
-    scores(X_)
-    shift(X_)
-    wait("v", "lv", 16)
-    V(g.vector.quantize_mx(T.vc[:], T.vx[:], T.vt[:]))
-    scores(PAR_)
-    shift(PAR_)
-    clamp(X_)
-    scores(Y_, [("vv", n_T[PAR_])])
-    pack(X_)
-    shift(Y_)
-    sums(X_)
-    clamp(Y_)
-    pack(Y_)
-    scores(OWN_, [("vv", n_lt[X_]), ("ss", n_ev[X_])])
-    clamp(PAR_)
-    sums(Y_)
-    pack(PAR_)
-    shift(OWN_)
-    sums(PAR_)
-    clamp(OWN_)
-    pack(OWN_)
+    def values(k):
+        wait("v", "lv", 16)
+        V(g.vector.quantize_mx(T.vc[:], T.vx[:], T.vt[:]))
 
-    def ready(k):
+    def out_c(k):
+        n = V(g.vector.transpose(T.ct[0:32, 0:32], T.cn[0:32, 0:32]))
+        wait("v", "vv", n)
+        n = V(g.vector.tensor_scalar(T.cu[0:32, :], T.ct[0:32, :], -1.0, None, Op.mult))
+        wait("y", "vv", n)
+        g.sync.dma_start(T.c[:], T.cu[0:16, :]).then_inc(S.out, 16)
+
+    steps = {"S": scores, "h": shift, "c": clamp, "p": pack, "u": sums, "v": values, "C": out_c}
+    for s in plan["steps"].split():
+        steps[s[0]](int(s[1:] or 0))
+
+    far0 = 4 * min(FG, FN)
+    far = T.cn[:, far0:far0 + 8]
+
+    def result(k, r, dst, sem):
         wait("g", "vv", n_lc[k])
         wait("g", "ss", n_ev[k])
+        send(T["st%d" % k][:], [(r, dst)], sem)
 
-    def land(r, s):
-        return T["al%d" % order_of(r).index(s)]
-
-    if is_gate:
-        wait("g", "vv", n_neg[PAR_])
-        send(cneg(PAR_), [(PAR, T.cpl[:])], "cp")
-        ready(X_)
-        wait("g", "ss", n_cc[X_])
-        send(T.st2[:], [(FG, land(FG, rank)[:])], "am%d" % rank)
-        wait("g", "ss", n_cc[Y_])
-        wait("g", "rc", ne)
-        send(T.cyb[:, 0:8], [(FN, T.cyl[:])], "cyl")
-        wait("g", "rx", ne)
-        send(T.fx[:], [(FG, land(FG, PAR)[:])], "am%d" % PAR)
-        ready(Y_)
-        send(T.st3[:, 0:132], [(FN, land(FN, rank)[:, 0:132])], "am%d" % rank)
-        wait("g", "ry", ne)
-        send(T.fy[:, 0:132], [(FN, land(FN, PAR)[:, 0:132])], "am%d" % PAR)
-    else:
-        wait("g", "ss", n_cc[Y_])
-        send(T.cys[:], [(PAR, T.cyb[:, 4:12])], "rc")
-        ready(X_)
-        send(T.st2[:], [(PAR, T.fx[:])], "rx")
-        ready(Y_)
-        send(T.st3[:, 0:132], [(PAR, T.fy[:, 0:132])], "ry")
-    ready(PAR_)
-    send(T.st1[:, 0:132], [(PAR, land(PAR, rank)[:, 0:132])], "am%d" % rank)
-
-    n = V(g.vector.transpose(T.ct[0:32, 0:32], T.cn[0:32, 0:32]))
-    wait("v", "vv", n)
-    n = V(g.vector.tensor_scalar(T.cu[0:32, :], T.ct[0:32, :], -1.0, None, Op.mult))
-    wait("y", "vv", n)
-    g.sync.dma_start(T.c[:], T.cu[0:16, :]).then_inc(S.out, 16)
-    sums(OWN_)
+    for s in plan["sends"]:
+        if s == "c neighbour":
+            wait("g", "vv", n_neg[PAR_])
+            send(cneg(PAR_), [(PAR, T.cpl[:])], "cp")
+        elif s == "c far":
+            wait("g", "vv", max(n_neg[X_], n_neg[Y_]))
+            if is_gate:
+                send(far, [(FN, T.cyl[:, 0:8]), (FG, T.cyl[:, 0:8])], "cyl")
+            else:
+                send(far, [(PAR, T.fc[:])], "rc")
+        elif s == "A neighbour":
+            result(PAR_, PAR, land(PAR, rank), "am%d" % rank)
+        elif s == "A far gate":
+            result(X_, *((FG, land(FG, rank), "am%d" % rank) if is_gate else (PAR, T.fx[:], "rx")))
+        elif s == "A far neighbour":
+            result(Y_, *((FN, land(FN, rank), "am%d" % rank) if is_gate else (PAR, T.fy[:], "ry")))
+        elif s == "pass c":
+            wait("g", "rc", ne)
+            send(T.fc[:], [(FN, T.cyl[:, 8:16]), (FG, T.cyl[:, 8:16])], "cyl")
+        elif s == "pass far gate":
+            wait("g", "rx", ne)
+            send(T.fx[:], [(FG, land(FG, PAR))], "am%d" % PAR)
+        elif s == "pass far neighbour":
+            wait("g", "ry", ne)
+            send(T.fy[:], [(FN, land(FN, PAR))], "am%d" % PAR)
 
     def tiny(j):
         return T.tiny[:, 4 * j:4 * j + 4]
 
-    if is_gate:
-        wait("v", "rc", ne)
-        wait("v", "am%d" % FG, ne)
-        wait("v", "am%d" % FN, ne)
-        neg = {PAR: T.cyb[:, 8:12], FG: T.al2[:, 132:136], FN: T.al3[:, 132:136]}
-    else:
-        wait("v", "cp", ne)
-        wait("v", "cyl", ne)
-        neg = {PAR: T.cpl[:], FG: T.cyl[:, 0:4], FN: T.cyl[:, 4:8]}
-    neg[rank] = cneg(OWN_)
+    wait("v", "cp", ne)
+    wait("v", "cyl", 2 * ne)
+    me = 4 * (rank - min(gate, nbr))
+    neg = {rank: cneg(OWN_), PAR: T.cpl[:], FG: T.cyl[:, me:me + 4], FN: T.cyl[:, 8 + me:12 + me]}
     V(g.vector.tensor_tensor(tiny(0), neg[rank], neg[PAR], Op.min))
     n = V(g.vector.tensor_tensor(tiny(1), neg[FG], neg[FN], Op.min))
     wait("v", "vv", n)
@@ -316,12 +325,9 @@ def rank_program(g, core, T, topo):
     wait("y", "vv", n_w)
     g.sync.dma_start(T.w[:], T.wr[0:1, :]).then_inc(S.out, 16)
 
-    def num(j):
-        return T.num[:, 128 * j:128 * j + 128]
-
     src = {rank: T.st0, PAR: T.al1, FG: T.al2, FN: T.al3}
     den = acc = None
-    arrive = [FG, FN, rank, PAR] if is_gate else [rank, FG, PAR, FN]
+    arrive = [rank, PAR, FG, FN] if not is_gate else [rank, FG, FN, PAR]
     for j, r in enumerate(arrive):
         if r == rank:
             wait("v", "ss", n_ev[OWN_])
@@ -329,16 +335,16 @@ def rank_program(g, core, T, topo):
             wait("v", "am%d" % r, ne)
         nd = V(g.vector.tensor_tensor(tiny(4 + 2 * j), src[r][:, 128:132], T.zw[:, 128 * r:128 * r + 128:32], Op.mult))
         wait("v", "vv", max(n_w, n_lc[OWN_]))
-        nn = V(g.vector.tensor_tensor(num(2 * j), src[r][:, 0:128], T.wr[:, 128 * r:128 * r + 128], Op.mult))
+        nn = V(g.vector.tensor_tensor(words(T.num, 2 * j), src[r][:, 0:128], words(T.wr, r), Op.mult))
         if j:
             wait("v", "vv", nd)
             nd = V(g.vector.tensor_tensor(tiny(5 + 2 * j), den, tiny(4 + 2 * j), Op.add))
             den = tiny(5 + 2 * j)
             wait("v", "vv", nn)
-            nn = V(g.vector.tensor_tensor(num(2 * j + 1), acc, num(2 * j), Op.add))
-            acc = num(2 * j + 1)
+            nn = V(g.vector.tensor_tensor(words(T.num, 2 * j + 1), acc, words(T.num, 2 * j), Op.add))
+            acc = words(T.num, 2 * j + 1)
         else:
-            den, acc = tiny(4), num(0)
+            den, acc = tiny(4), words(T.num, 0)
     wait("v", "vv", nd)
     nr = V(g.vector.reciprocal(T.zr[:, 0:128:32], den))
     wait("v", "vv", nr)

@@ -19,11 +19,10 @@ SCRATCH = {
     "r0": ("sbuf", [128, 16], F), "r1": ("sbuf", [128, 16], F), "r2": ("sbuf", [128, 16], F),
     "lt": ("sbuf", [128, 512], F),
     "fx": ("sbuf", [128, 132], F), "fy": ("sbuf", [128, 132], F), "fc": ("sbuf", [128, 8], F),
-    "cyl": ("sbuf", [128, 16], F), "cpl": ("sbuf", [128, 4], F),
-    "mask": ("sbuf", [128, 512], F), "zw": ("sbuf", [128, 512], F), "wb": ("sbuf", [128, 512], F),
-    "wr": ("sbuf", [128, 512], F), "zr": ("sbuf", [128, 128], F), "rb": ("sbuf", [128, 128], F),
-    "rw": ("sbuf", [128, 128], F), "dd": ("sbuf", [128, 16], F), "tiny": ("sbuf", [128, 64], F),
-    "num": ("sbuf", [128, 1024], F), "res": ("sbuf", [128, 128], F),
+    "cyl": ("sbuf", [128, 8], F), "cpl": ("sbuf", [128, 4], F),
+    "dd": ("sbuf", [128, 16], F), "ww": ("sbuf", [128, 32], F), "wt": ("sbuf", [128, 32], F),
+    "tiny": ("sbuf", [128, 64], F), "num": ("sbuf", [128, 1024], F), "rt": ("sbuf", [128, 128], F),
+    "res": ("sbuf", [128, 128], F),
     "ps0": ("psum", [128, 2048], F), "ps1": ("psum", [128, 2048], F),
 }
 for _k in range(4):
@@ -33,8 +32,8 @@ for _k in range(4):
     SCRATCH["et%d" % _k] = ("sbuf", [128, 512], B)
     if _k:
         SCRATCH["al%d" % _k] = ("sbuf", [128, 132], F)
-SEMAPHORES = (["vv", "tt", "ss", "lq", "lv", "out", "rx", "ry", "rc", "cp", "cyl", "ls"]
-              + ["lk%d" % r for r in range(4)] + ["qa%d" % r for r in range(4)] + ["am%d" % r for r in range(4)])
+SEMAPHORES = (["vv", "tt", "ss", "lq", "lv", "out", "rx", "ry", "rcx", "rcy", "cp", "cyl", "ls"]
+              + [s + "%d" % r for s in ("lk", "qa", "qb", "am") for r in range(4)])
 
 SCALE = float(np.float32(0.0125))
 FLOOR = float(np.float32(np.exp(-20.0)))
@@ -42,23 +41,22 @@ FLOOR = float(np.float32(np.exp(-20.0)))
 PLAN_GATE = {
     "steps": "S0 h0 v S1 h1 c1 S2 p1 h2 u1 c2 S3 p2 h3 u2 c3 p3 c0 u3 p0 u0 C",
     "sets": {0: 0, 1: 1, 2: 0, 3: 1}, "al": {0: (0, 2), 1: (1, 0), 2: (0, 0), 3: (1, 0)},
-    "sends": ["c neighbour", "A neighbour", "c far", "A far gate", "pass c", "pass far gate", "A far neighbour",
-              "pass far neighbour"],
+    "sends": ["c1", "A1", "c2", "c3", "A2", "A3"],
 }
 PLAN_NEIGHBOUR = {
     "steps": "S0 h0 S2 h2 v c2 S3 p2 h3 u2 c3 p3 S1 c0 u3 h1 c1 p1 p0 u1 u0 C",
     "sets": {0: 1, 1: 0, 2: 0, 3: 1}, "al": {0: (1, 2), 1: (0, 0), 2: (0, 0), 3: (1, 0)},
-    "sends": ["c far", "A far gate", "A far neighbour", "c neighbour", "A neighbour"],
+    "sends": ["c2", "c3", "A2", "A3", "c1", "A1"],
 }
 
 
 def rank_program(g, core, T, topo):
-    rank = T.rank_of(core)
-    if rank is None:
-        return
     S = T.sem
     cores = T.cores
     n_ranks = len(cores)
+    rank = T.rank_of(core)
+    if all(topo.chip(core) != topo.chip(c) for c in cores):
+        return
     Op, Fn, AX = AluOpType, ActivationFunctionType, AxisListType.X
 
     def gate_of(c):
@@ -73,9 +71,13 @@ def rank_program(g, core, T, topo):
         return [r, nb if r == ga else ga, fg, fn]
 
     gate, nbr, away = gate_of(core)
+    helper = [c for c in range(topo.CHIPS * topo.CORES_PER_CHIP) if topo.chip(c) == topo.chip(core) and c not in cores
+              and topo.die(c) == topo.die(cores[nbr]) and all(topo.may_write(c, cores[r]) for r in away)][0]
+    if rank is None and core != helper:
+        return
     is_gate = rank == gate
     plan = PLAN_GATE if is_gate else PLAN_NEIGHBOUR
-    order = order_of(rank)
+    order = order_of(nbr if rank is None else rank)
     _, PAR, FG, FN = order
     OWN_, PAR_, X_, Y_ = 0, 1, 2, 3
     lanes = topo.mask(core, cores[FG])
@@ -106,20 +108,11 @@ def rank_program(g, core, T, topo):
 
     sent = [0]
 
-    def send(src, dsts, sem):
-        ids = []
-        for r, _ in dsts:
-            rid, pid, _s = topo.addr(cores[r])
-            ids.append(DstId(rid=rid, pnc=pid))
-        g.remote_dma_fused([RemoteDMATransfer(dst_ids=ids, dma_engine_mask=lanes, remote_sem=T.sem[sem], srcs=[src],
-                                              dsts=[d for _, d in dsts])], local_sem=T.sem["ls"])
+    def send(src, dst_core, dst, sem):
+        rid, pid, _s = topo.addr(dst_core)
+        g.remote_dma_fused([RemoteDMATransfer(dst_ids=[DstId(rid=rid, pnc=pid)], dma_engine_mask=lanes,
+                                              remote_sem=T.sem[sem], srcs=[src], dsts=[dst])], local_sem=T.sem["ls"])
         sent[0] += ne
-
-    def codes(slot):
-        return T.qc[:, 128 * slot:128 * slot + 128].bitcast(dt.uint8)
-
-    def scales(slot):
-        return T.qx[:, 128 * slot:128 * slot + 128]
 
     def slot_at(r, s):
         return order_of(r).index(s)
@@ -127,11 +120,14 @@ def rank_program(g, core, T, topo):
     def land(r, s):
         return T["al%d" % slot_at(r, s)][:]
 
-    def send_q(s, to):
-        k = slot_at(rank, s)
-        for r in to:
-            send(codes(k), [(r, codes(slot_at(r, s)))], "qa%d" % s)
-            send(scales(k), [(r, scales(slot_at(r, s)))], "qa%d" % s)
+    if rank is None:
+        for sem, src, to, dst, arrive in (
+                ("rcx", T.fc[:, 0:4], FG, T.cyl[:, 4:8], "cyl"), ("rcy", T.fc[:, 4:8], FN, T.cyl[:, 4:8], "cyl"),
+                ("rx", T.fx[:], FG, land(FG, nbr), "am%d" % nbr), ("ry", T.fy[:], FN, land(FN, nbr), "am%d" % nbr)):
+            wait("g", sem, ne)
+            send(src, cores[to], dst, arrive)
+        wait("g", "ls", sent[0])
+        return
 
     g.sync.dma_start(T.qt[:], T.q[:]).then_inc(S.lq, 16)
     for h in range(4):
@@ -139,23 +135,29 @@ def rank_program(g, core, T, topo):
     g.sync.dma_start(T.vt[:], T.v[:]).then_inc(S.lv, 16)
 
     n_ot = V(g.vector.memset(T.ot[:], 1.0))
-    n_mask = V(g.vector.memset(T.mask[:], 1.0))
-    V(g.vector.memset(T.zr[:], 0.0))
+    V(g.vector.memset(T.ww[:, 16:32], 0.0))
     V(g.vector.memset(T.cn[:, 16:32], 0.0))
     wait("v", "lq", 16)
     n_q = V(g.vector.quantize_mx(T.qc[:, 0:128], T.qx[:, 0:128], T.qt[:]))
     wait("v", "vv", n_ot)
     V(g.vector.quantize_mx(T.oc[:], T.ox[:], T.ot[:]))
-    wait("v", "vv", n_mask)
-    V(g.vector.memset(T.mask[:, 0:512:32], 0.0))
-    n_zero = V(g.vector.memset(T.zw[:], 0.0))
+
+    def send_q(s, r):
+        i, o = 128 * slot_at(rank, s), 128 * slot_at(r, s)
+        if s != rank:
+            wait("g", "qa%d" % s, ne)
+        send(T.qc[:, i:i + 128].bitcast(dt.uint8), cores[r], T.qc[:, o:o + 128].bitcast(dt.uint8), "qa%d" % s)
+        if s != rank:
+            wait("g", "qb%d" % s, ne)
+        send(T.qx[:, i:i + 128], cores[r], T.qx[:, o:o + 128], "qb%d" % s)
 
     wait("g", "vv", n_q)
     if is_gate:
-        send_q(rank, [FN, FG])
-        wait("g", "qa%d" % PAR, 2 * ne)
-        send_q(PAR, [FN, FG])
-    send_q(rank, [PAR])
+        send_q(rank, FN)
+        send_q(rank, FG)
+        send_q(PAR, FN)
+        send_q(PAR, FG)
+    send_q(rank, PAR)
 
     n_k = []
     for h in range(4):
@@ -167,18 +169,18 @@ def rank_program(g, core, T, topo):
     psum = [T.ps0, T.ps1]
     holds = {}
 
-    def bank(at, taker):
-        if at in holds:
-            wait("t", *holds[at]())
-        holds[at] = taker
+    def view(at):
         return psum[at[0]][:, 512 * at[1]:512 * at[1] + 128]
+
+    def bank(at, freed):
+        if at in holds:
+            wait("t", "vv", holds[at]())
+        holds[at] = freed
+        return view(at)
 
     def where(k, j):
         s, b = plan["al"][k]
         return s, b + j
-
-    def view(at):
-        return psum[at[0]][:, 512 * at[1]:512 * at[1] + 128]
 
     def words(buf, k):
         return buf[:, 128 * k:128 * k + 128]
@@ -187,10 +189,11 @@ def rank_program(g, core, T, topo):
         if k == OWN_:
             wait("t", "vv", n_q)
         else:
-            wait("t", "qa%d" % order[k], 2 * ne)
+            wait("t", "qa%d" % order[k], ne)
+            wait("t", "qb%d" % order[k], ne)
         n_S[k] = []
         for b in range(4):
-            out = bank((plan["sets"][k], b), lambda k=k, b=b: ("vv", n_T[k][b]))
+            out = bank((plan["sets"][k], b), lambda k=k, b=b: n_T[k][b])
             wait("t", "vv", n_k[b])
             n_S[k].append(M(g.tensor.matmul_mx(out, words(T.kc, b), words(T.kx, b), words(T.qc, k), words(T.qx, k),
                                                True, True)))
@@ -209,11 +212,11 @@ def rank_program(g, core, T, topo):
         lo, hi = 4 * k, 4 * k + 4
         for b in range(4):
             n = V(g.vector.tensor_reduce(T.r0[:, lo + b:lo + b + 1], t1[:, 128 * b:128 * b + 128], AX, Op.max, negate=True))
-        for src, dst, step in ((T.r0, T.r1, 64), (T.r1, T.r2, 32)):
+        for src, dst, parts in ((T.r0, T.r1, ((0, 0, 64, 64), (64, 32, 96, 32), (96, 0, 64, 32))),
+                                (T.r1, T.r2, ((0, 0, 64, 64), (64, 0, 64, 64)))):
             wait("v", "vv", n)
-            for a in range(0, 128, step):
-                o = a ^ step
-                n = V(g.vector.tensor_tensor(dst[a:a + step, lo:hi], src[a:a + step, lo:hi], src[o:o + step, lo:hi], Op.min))
+            for o, a, b, m in parts:
+                n = V(g.vector.tensor_tensor(dst[o:o + m, lo:hi], src[a:a + m, lo:hi], src[b:b + m, lo:hi], Op.min))
         wait("v", "vv", n)
         n_neg[k] = V(g.vector.tensor_scalar(cneg(k), T.r2[:, lo:hi], SCALE, None, Op.mult))
         wait("s", "vv", n_neg[k])
@@ -240,16 +243,16 @@ def rank_program(g, core, T, topo):
         wait("y", "vv", n)
         g.sync.dma_start(T.p[order[k]], P[:]).then_inc(S.out, 16)
         wait("t", "vv", n_pq[k])
-        out = bank(where(k, 1), lambda k=k: ("vv", n_lt[k]))
+        out = bank(where(k, 1), lambda k=k: n_lt[k])
         n_L[k] = M(g.tensor.matmul_mx(out, T.oc[:], T.ox[:], words(T.pc, k), words(T.px, k), True, True))
-        out = bank(where(k, 0), lambda k=k: ("ss", n_ev[k]))
+        out = bank(where(k, 0), lambda k=k: n_ev[k])
         n_A[k] = M(g.tensor.matmul_mx(out, T.vc[:], T.vx[:], words(T.pc, k), words(T.px, k), True, True))
-        wait("s", "tt", n_A[k])
-        n_ev[k] = E(g.scalar.activation(T["st%d" % k][:, 0:128], view(where(k, 0)), Fn.Copy))
 
     def sums(k):
         wait("v", "tt", n_L[k])
         n_lt[k] = V(g.vector.transpose(words(T.lt, k), view(where(k, 1))))
+        wait("v", "tt", n_A[k])
+        n_ev[k] = V(g.vector.transpose(T["st%d" % k][:, 0:128], view(where(k, 0))))
         wait("v", "vv", n_lt[k])
         n_lc[k] = V(g.vector.tensor_copy(T["st%d" % k][:, 128:132], T.lt[:, 128 * k:128 * k + 128:32]))
 
@@ -268,47 +271,27 @@ def rank_program(g, core, T, topo):
     for s in plan["steps"].split():
         steps[s[0]](int(s[1:] or 0))
 
-    far0 = 4 * min(FG, FN)
-    far = T.cn[:, far0:far0 + 8]
-
-    def result(k, r, dst, sem):
-        wait("g", "vv", n_lc[k])
-        wait("g", "ss", n_ev[k])
-        send(T["st%d" % k][:], [(r, dst)], sem)
+    def road(k, what):
+        if k == PAR_:
+            return (cores[PAR],) + ((T.cpl[:], "cp") if what == "c" else (land(PAR, rank), "am%d" % rank))
+        if is_gate:
+            r = order[k]
+            return (cores[r],) + ((T.cyl[:, 0:4], "cyl") if what == "c" else (land(r, rank), "am%d" % rank))
+        if what == "c":
+            return (helper,) + ((T.fc[:, 0:4], "rcx") if k == X_ else (T.fc[:, 4:8], "rcy"))
+        return (helper,) + ((T.fx[:], "rx") if k == X_ else (T.fy[:], "ry"))
 
     for s in plan["sends"]:
-        if s == "c neighbour":
-            wait("g", "vv", n_neg[PAR_])
-            send(cneg(PAR_), [(PAR, T.cpl[:])], "cp")
-        elif s == "c far":
-            wait("g", "vv", max(n_neg[X_], n_neg[Y_]))
-            if is_gate:
-                send(far, [(FN, T.cyl[:, 0:8]), (FG, T.cyl[:, 0:8])], "cyl")
-            else:
-                send(far, [(PAR, T.fc[:])], "rc")
-        elif s == "A neighbour":
-            result(PAR_, PAR, land(PAR, rank), "am%d" % rank)
-        elif s == "A far gate":
-            result(X_, *((FG, land(FG, rank), "am%d" % rank) if is_gate else (PAR, T.fx[:], "rx")))
-        elif s == "A far neighbour":
-            result(Y_, *((FN, land(FN, rank), "am%d" % rank) if is_gate else (PAR, T.fy[:], "ry")))
-        elif s == "pass c":
-            wait("g", "rc", ne)
-            send(T.fc[:], [(FN, T.cyl[:, 8:16]), (FG, T.cyl[:, 8:16])], "cyl")
-        elif s == "pass far gate":
-            wait("g", "rx", ne)
-            send(T.fx[:], [(FG, land(FG, PAR))], "am%d" % PAR)
-        elif s == "pass far neighbour":
-            wait("g", "ry", ne)
-            send(T.fy[:], [(FN, land(FN, PAR))], "am%d" % PAR)
+        k = int(s[1])
+        wait("g", "vv", n_neg[k] if s[0] == "c" else max(n_lc[k], n_ev[k]))
+        send(cneg(k) if s[0] == "c" else T["st%d" % k][:], *road(k, s[0]))
 
     def tiny(j):
         return T.tiny[:, 4 * j:4 * j + 4]
 
     wait("v", "cp", ne)
     wait("v", "cyl", 2 * ne)
-    me = 4 * (rank - min(gate, nbr))
-    neg = {rank: cneg(OWN_), PAR: T.cpl[:], FG: T.cyl[:, me:me + 4], FN: T.cyl[:, 8 + me:12 + me]}
+    neg = {rank: cneg(OWN_), PAR: T.cpl[:], FG: T.cyl[:, 0:4], FN: T.cyl[:, 4:8]}
     V(g.vector.tensor_tensor(tiny(0), neg[rank], neg[PAR], Op.min))
     n = V(g.vector.tensor_tensor(tiny(1), neg[FG], neg[FN], Op.min))
     wait("v", "vv", n)
@@ -316,44 +299,51 @@ def rank_program(g, core, T, topo):
     wait("v", "vv", n)
     for j in order:
         n = V(g.vector.tensor_tensor(T.dd[:, 4 * j:4 * j + 4], tiny(2), neg[j], Op.subtract))
-    wait("s", "vv", max(n, n_zero))
-    nx = E(g.scalar.activation(T.zw[:, 0:512:32], T.dd[:], Fn.Exp))
-    wait("v", "ss", nx)
-    n = V(g.vector.tensor_tensor_scan(T.wb[:], T.mask[:], T.zw[:], 0.0, Op.mult, Op.add))
-    wait("v", "vv", n)
-    n_w = V(g.vector.transpose(T.wr[:], T.wb[:]))
-    wait("y", "vv", n_w)
-    g.sync.dma_start(T.w[:], T.wr[0:1, :]).then_inc(S.out, 16)
+    wait("s", "vv", n)
+    nx = E(g.scalar.activation(T.ww[:, 0:16], T.dd[:], Fn.Exp))
 
     src = {rank: T.st0, PAR: T.al1, FG: T.al2, FN: T.al3}
-    den = acc = None
-    arrive = [rank, PAR, FG, FN] if not is_gate else [rank, FG, FN, PAR]
+    arrive = [rank, FG, FN, PAR] if is_gate else [rank, PAR, FG, FN]
+    den, acc, nn = None, None, 0
     for j, r in enumerate(arrive):
-        if r == rank:
-            wait("v", "ss", n_ev[OWN_])
+        last = j == len(arrive) - 1
+        if j == 0:
+            wait("s", "ss", nx)
+        else:
+            wait("s", "am%d" % r, ne)
+        for b in range(4):
+            c = 256 * j + 32 * b
+            ns = E(g.scalar.activation(T.num[:, c:c + 32], src[r][:, 32 * b:32 * b + 32], Fn.Copy,
+                                       scale=T.ww[:, 4 * r + b:4 * r + b + 1]))
+        if j == 0:
+            wait("v", "ss", nx)
+            n = V(g.vector.transpose(T.wt[0:32, 0:32], T.ww[0:32, 0:32]))
+            wait("y", "vv", n)
+            g.sync.dma_start(T.w[:], T.wt[0:16, :]).then_inc(S.out, 16)
         else:
             wait("v", "am%d" % r, ne)
-        nd = V(g.vector.tensor_tensor(tiny(4 + 2 * j), src[r][:, 128:132], T.zw[:, 128 * r:128 * r + 128:32], Op.mult))
-        wait("v", "vv", max(n_w, n_lc[OWN_]))
-        nn = V(g.vector.tensor_tensor(words(T.num, 2 * j), src[r][:, 0:128], words(T.wr, r), Op.mult))
-        if j:
-            wait("v", "vv", nd)
-            nd = V(g.vector.tensor_tensor(tiny(5 + 2 * j), den, tiny(4 + 2 * j), Op.add))
-            den = tiny(5 + 2 * j)
-            wait("v", "vv", nn)
-            nn = V(g.vector.tensor_tensor(words(T.num, 2 * j + 1), acc, words(T.num, 2 * j), Op.add))
-            acc = words(T.num, 2 * j + 1)
-        else:
+        nd = V(g.vector.tensor_tensor(tiny(4 + 2 * j), src[r][:, 128:132], T.ww[:, 4 * r:4 * r + 4], Op.mult))
+        if j == 0:
             den, acc = tiny(4), words(T.num, 0)
-    wait("v", "vv", nd)
-    nr = V(g.vector.reciprocal(T.zr[:, 0:128:32], den))
-    wait("v", "vv", nr)
-    nr = V(g.vector.tensor_tensor_scan(T.rb[:], T.mask[:, 0:128], T.zr[:], 0.0, Op.mult, Op.add))
-    wait("v", "vv", nr)
-    nr = V(g.vector.transpose(T.rw[:], T.rb[:]))
-    wait("v", "vv", nr)
-    nr = V(g.vector.tensor_tensor(T.res[:], acc, T.rw[:], Op.mult))
-    wait("y", "vv", nr)
+            continue
+        wait("v", "vv", nd)
+        nd = V(g.vector.tensor_tensor(tiny(5 + 2 * j), den, tiny(4 + 2 * j), Op.add))
+        den = tiny(5 + 2 * j)
+        if last:
+            wait("v", "vv", nd)
+            nd = V(g.vector.reciprocal(tiny(3), den))
+        wait("v", "ss", ns)
+        wait("v", "vv", nn)
+        nn = V(g.vector.tensor_tensor(words(T.num, 2 * j + 1), acc, words(T.num, 2 * j), Op.add))
+        acc = words(T.num, 2 * j + 1)
+    wait("v", "vv", max(nd, nn))
+    o = 128 * (2 * len(arrive) - 1)
+    for b in range(4):
+        n = V(g.vector.tensor_scalar(T.rt[:, 32 * b:32 * b + 32], T.num[:, o + 32 * b:o + 32 * b + 32],
+                                     T.tiny[:, 12 + b:13 + b], None, Op.mult))
+    wait("v", "vv", n)
+    n = V(g.vector.transpose(T.res[:], T.rt[:]))
+    wait("y", "vv", n)
     g.sync.dma_start(T.o[:], T.res[:]).then_inc(S.out, 16)
     g.sync.wait_ge(S.out, 16 * 7)
     wait("g", "ss", tick["ss"])

@@ -6,47 +6,51 @@ F = "float32"
 B = "bfloat16"
 C4 = "float8_e4m3fn_x4"
 U8 = "uint8"
+W = 129
 SCRATCH = {
     "qt": ("sbuf", [128, 512], B), "kt": ("sbuf", [128, 2048], B), "vt": ("sbuf", [128, 512], B),
     "ot": ("sbuf", [128, 512], B),
     "qc": ("sbuf", [128, 512], C4), "qx": ("sbuf", [128, 512], U8),
     "kc": ("sbuf", [128, 512], C4), "kx": ("sbuf", [128, 512], U8),
-    "vc": ("sbuf", [128, 128], C4), "vx": ("sbuf", [128, 128], U8),
-    "oc": ("sbuf", [128, 128], C4), "ox": ("sbuf", [128, 128], U8),
+    "vc": ("sbuf", [128, 256], C4), "vx": ("sbuf", [128, 256], U8),
     "pc": ("sbuf", [128, 512], C4), "px": ("sbuf", [128, 512], U8),
-    "cn": ("sbuf", [128, 32], F),
-    "ct": ("sbuf", [128, 32], F), "cu": ("sbuf", [128, 32], F),
-    "r0": ("sbuf", [128, 16], F), "r1": ("sbuf", [128, 16], F), "r2": ("sbuf", [128, 16], F),
-    "lt": ("sbuf", [128, 512], F),
-    "fx": ("sbuf", [128, 132], F), "fy": ("sbuf", [128, 132], F), "fc": ("sbuf", [128, 8], F),
-    "cyl": ("sbuf", [128, 8], F), "cpl": ("sbuf", [128, 4], F),
-    "dd": ("sbuf", [128, 16], F), "ww": ("sbuf", [128, 32], F), "wt": ("sbuf", [128, 32], F),
-    "tiny": ("sbuf", [128, 64], F), "num": ("sbuf", [128, 1024], F), "rt": ("sbuf", [128, 128], F),
-    "res": ("sbuf", [128, 128], F),
-    "ps0": ("psum", [128, 2048], F), "ps1": ("psum", [128, 2048], F),
+    "m20": ("sbuf", [128, 8], F), "fl": ("sbuf", [128, 8], B),
+    "rm": ("sbuf", [128, 16], F), "cn": ("sbuf", [128, 16], F),
+    "cw": ("sbuf", [128, 32], F), "cwt": ("sbuf", [128, 32], F),
+    "cl": ("sbuf", [128, 16], F), "mn": ("sbuf", [128, 4], F), "ri": ("sbuf", [128, 4], F),
+    "fx": ("sbuf", [128, W], F), "fy": ("sbuf", [128, W], F), "fc": ("sbuf", [128, 8], F),
+    "rt": ("sbuf", [128, 128], F), "res": ("sbuf", [128, 128], F),
+    "ps": ("psum", [128, 2048], F), "pa": ("psum", [128, 2048], F),
 }
 for _k in range(4):
+    SCRATCH["en%d" % _k] = ("sbuf", [128, 4, 128], B)
+    SCRATCH["et%d" % _k] = ("sbuf", [128, 4, 128], B)
     SCRATCH["p%d" % _k] = ("sbuf", [128, 512], B)
-    SCRATCH["st%d" % _k] = ("sbuf", [128, 132], F)
-    SCRATCH["t1_%d" % _k] = ("sbuf", [128, 512], F)
-    SCRATCH["et%d" % _k] = ("sbuf", [128, 512], B)
+    SCRATCH["nu%d" % _k] = ("sbuf", [128, W], F)
     if _k:
-        SCRATCH["al%d" % _k] = ("sbuf", [128, 132], F)
+        SCRATCH["st%d" % _k] = ("sbuf", [128, W], F)
+        SCRATCH["al%d" % _k] = ("sbuf", [128, W], F)
+        SCRATCH["ac%d" % _k] = ("sbuf", [128, W], F)
 SEMAPHORES = (["vv", "tt", "ss", "lq", "lv", "out", "rx", "ry", "rcx", "rcy", "cp", "cyl", "ls"]
               + [s + "%d" % r for s in ("lk", "qa", "qb", "am") for r in range(4)])
 
 SCALE = float(np.float32(0.0125))
-FLOOR = float(np.float32(np.exp(-20.0)))
 
 PLAN_GATE = {
-    "steps": "S0 h0 v S1 h1 c1 S2 p1 h2 u1 c2 S3 p2 h3 u2 c3 p3 c0 u3 p0 u0 C",
-    "sets": {0: 0, 1: 1, 2: 0, 3: 1}, "al": {0: (0, 2), 1: (1, 0), 2: (0, 0), 3: (1, 0)},
-    "sends": ["c1", "A1", "c2", "c3", "A2", "A3"],
+    "t": "S0 S1 S2 S3 A1 A2 A3 A0",
+    "v": "r0 x0 r1 c0 v r2 c1 p0 x1 p1 r3 c2 x2 p2 x3 c3 p3",
+    "s": "e0 x0 e1 x1 e2 x2 e3 a1 x3 a2 a3",
+    "q": "FN FG PAR RFN RFG",
+    "by": [1, 2, 3, 2],
+    "sends": "c2 c1 A1 A2 c3 A3",
 }
 PLAN_NEIGHBOUR = {
-    "steps": "S0 h0 S2 h2 v c2 S3 p2 h3 u2 c3 p3 S1 c0 u3 h1 c1 p1 p0 u1 u0 C",
-    "sets": {0: 1, 1: 0, 2: 0, 3: 1}, "al": {0: (1, 2), 1: (0, 0), 2: (0, 0), 3: (1, 0)},
-    "sends": ["c2", "c3", "A2", "A3", "c1", "A1"],
+    "t": "S0 S2 S1 S3 A0 A2 A3 A1",
+    "v": "r0 r2 c0 x0 p0 x2 v r3 r1 c2 p2 x3 c3 p3 x1 c1 p1",
+    "s": "e0 x0 e2 x2 e3 x3 e1 a2 x1 a3 a1",
+    "q": "PAR",
+    "by": [3, 1, 1, 1],
+    "sends": "c2 c3 c1 A2 A3 A1",
 }
 
 
@@ -120,9 +124,12 @@ def rank_program(g, core, T, topo):
     def land(r, s):
         return T["al%d" % slot_at(r, s)][:]
 
+    def shift_of(r):
+        return T.cl[:, 4 * r:4 * r + 1]
+
     if rank is None:
         for sem, src, to, dst, arrive in (
-                ("rcx", T.fc[:, 0:4], FG, T.cyl[:, 4:8], "cyl"), ("rcy", T.fc[:, 4:8], FN, T.cyl[:, 4:8], "cyl"),
+                ("rcx", T.fc[:, 0:1], FG, shift_of(nbr), "cyl"), ("rcy", T.fc[:, 4:5], FN, shift_of(nbr), "cyl"),
                 ("rx", T.fx[:], FG, land(FG, nbr), "am%d" % nbr), ("ry", T.fy[:], FN, land(FN, nbr), "am%d" % nbr)):
             wait("g", sem, ne)
             send(src, cores[to], dst, arrive)
@@ -134,13 +141,15 @@ def rank_program(g, core, T, topo):
         g.sync.dma_start(T.kt[:, 512 * h:512 * h + 512], T.k[:, 512 * h:512 * h + 512]).then_inc(T.sem["lk%d" % h], 16)
     g.sync.dma_start(T.vt[:], T.v[:]).then_inc(S.lv, 16)
 
+    n_m20 = V(g.vector.memset(T.m20[:], -20.0))
     n_ot = V(g.vector.memset(T.ot[:], 1.0))
-    V(g.vector.memset(T.ww[:, 16:32], 0.0))
-    V(g.vector.memset(T.cn[:, 16:32], 0.0))
+    V(g.vector.memset(T.cw[:, 8:32], 0.0))
+    wait("s", "vv", n_m20)
+    n_fl = E(g.scalar.activation(T.fl[:], T.m20[:], Fn.Exp))
     wait("v", "lq", 16)
     n_q = V(g.vector.quantize_mx(T.qc[:, 0:128], T.qx[:, 0:128], T.qt[:]))
     wait("v", "vv", n_ot)
-    V(g.vector.quantize_mx(T.oc[:], T.ox[:], T.ot[:]))
+    V(g.vector.quantize_mx(T.vc[:, 128:256], T.vx[:, 128:256], T.ot[:]))
 
     def send_q(s, r):
         i, o = 128 * slot_at(rank, s), 128 * slot_at(r, s)
@@ -152,200 +161,176 @@ def rank_program(g, core, T, topo):
         send(T.qx[:, i:i + 128], cores[r], T.qx[:, o:o + 128], "qb%d" % s)
 
     wait("g", "vv", n_q)
-    if is_gate:
-        send_q(rank, FN)
-        send_q(rank, FG)
-        send_q(PAR, FN)
-        send_q(PAR, FG)
-    send_q(rank, PAR)
+    for step in plan["q"].split():
+        send_q(*{"FN": (rank, FN), "FG": (rank, FG), "PAR": (rank, PAR), "RFN": (PAR, FN), "RFG": (PAR, FG)}[step])
 
-    n_k = []
     for h in range(4):
         wait("v", "lk%d" % h, 16)
-        n_k.append(V(g.vector.quantize_mx(T.kc[:, 128 * h:128 * h + 128], T.kx[:, 128 * h:128 * h + 128],
-                                          T.kt[:, 512 * h:512 * h + 512])))
+        n_k = V(g.vector.quantize_mx(T.kc[:, 128 * h:128 * h + 128], T.kx[:, 128 * h:128 * h + 128],
+                                     T.kt[:, 512 * h:512 * h + 512]))
 
-    n_S, n_T, n_neg, n_exp, n_P, n_pq, n_L, n_A, n_lt, n_lc, n_ev = {}, {}, {}, {}, {}, {}, {}, {}, {}, {}, {}
-    psum = [T.ps0, T.ps1]
-    holds = {}
-
-    def view(at):
-        return psum[at[0]][:, 512 * at[1]:512 * at[1] + 128]
-
-    def bank(at, freed):
-        if at in holds:
-            wait("t", "vv", holds[at]())
-        holds[at] = freed
-        return view(at)
-
-    def where(k, j):
-        s, b = plan["al"][k]
-        return s, b + j
+    n_S, n_A, n_r, n_c, n_e, n_xs, n_xv, n_P, n_pq, n_a, n_v = {}, {}, {}, {}, {}, {}, {}, {}, {}, {}, {}
 
     def words(buf, k):
         return buf[:, 128 * k:128 * k + 128]
 
     def scores(k):
-        if k == OWN_:
-            wait("t", "vv", n_q)
-        else:
+        return T.ps[:, 512 * k:512 * k + 512]
+
+    def t_S(k):
+        wait("t", "vv", n_k)
+        if k != OWN_:
             wait("t", "qa%d" % order[k], ne)
             wait("t", "qb%d" % order[k], ne)
-        n_S[k] = []
-        for b in range(4):
-            out = bank((plan["sets"][k], b), lambda k=k, b=b: n_T[k][b])
-            wait("t", "vv", n_k[b])
-            n_S[k].append(M(g.tensor.matmul_mx(out, words(T.kc, b), words(T.kx, b), words(T.qc, k), words(T.qx, k),
-                                               True, True)))
+        n_S[k] = M(g.tensor.matmul_mx(scores(k), words(T.qc, k), words(T.qx, k), T.kc[:], T.kx[:], True, True))
+
+    def v_r(k):
+        wait("v", "tt", n_S[k])
+        n_r[k] = V(g.vector.tensor_reduce(T.rm[:, k:k + 1], scores(k), AX, Op.max, negate=True))
 
     def cneg(k):
-        return T.cn[:, 4 * order[k]:4 * order[k] + 4]
+        return T.cn[:, order[k]:order[k] + 1]
 
-    def shift(k):
-        t1 = T["t1_%d" % k]
-        et = T["et%d" % k]
-        n_T[k] = []
-        for b in range(4):
-            wait("v", "tt", n_S[k][b])
-            n_T[k].append(V(g.vector.transpose(t1[:, b:512:4], view((plan["sets"][k], b)))))
-        wait("v", "vv", n_T[k][3])
-        lo, hi = 4 * k, 4 * k + 4
-        for b in range(4):
-            n = V(g.vector.tensor_reduce(T.r0[:, lo + b:lo + b + 1], t1[:, 128 * b:128 * b + 128], AX, Op.max, negate=True))
-        for src, dst, parts in ((T.r0, T.r1, ((0, 0, 64, 64), (64, 32, 96, 32), (96, 0, 64, 32))),
-                                (T.r1, T.r2, ((0, 0, 64, 64), (64, 0, 64, 64)))):
-            wait("v", "vv", n)
-            for o, a, b, m in parts:
-                n = V(g.vector.tensor_tensor(dst[o:o + m, lo:hi], src[a:a + m, lo:hi], src[b:b + m, lo:hi], Op.min))
-        wait("v", "vv", n)
-        n_neg[k] = V(g.vector.tensor_scalar(cneg(k), T.r2[:, lo:hi], SCALE, None, Op.mult))
-        wait("s", "vv", n_neg[k])
-        n_exp[k] = []
-        c = 4 * order[k]
-        for b in range(4):
-            n_exp[k].append(E(g.scalar.activation(et[:, 128 * b:128 * b + 128], t1[:, 128 * b:128 * b + 128], Fn.Exp,
-                                                  bias=T.cn[:, c + b:c + b + 1], scale=SCALE)))
+    def s_e(k):
+        wait("s", "vv", n_r[k])
+        n_c[k] = E(g.scalar.activation(cneg(k), T.rm[:, k:k + 1], Fn.Copy, scale=SCALE))
+        wait("s", "ss", n_c[k])
+        n_e[k] = E(g.scalar.activation(T["en%d" % k][:, :, :], scores(k), Fn.Exp, bias=cneg(k), scale=SCALE))
 
-    def clamp(k):
-        et = T["et%d" % k]
-        for b in range(4):
-            wait("v", "ss", n_exp[k][b])
-            n_P[k] = V(g.vector.tensor_scalar(et[:, 128 * b:128 * b + 128], et[:, 128 * b:128 * b + 128], FLOOR, None, Op.max))
+    def block(buf, part, col):
+        return buf[32 * part:32 * part + 32, :, 32 * col:32 * col + 32]
 
-    def pack(k):
-        et = T["et%d" % k]
+    def s_x(k):
+        wait("s", "ss", n_e[k])
+        for kk in range(plan["by"][k]):
+            for a in range(4):
+                n_xs[k] = E(g.scalar.activation(block(T["et%d" % k], kk, a), block(T["en%d" % k], a, kk), Fn.Copy))
+
+    def v_x(k):
+        wait("v", "ss", n_e[k])
+        for kk in range(plan["by"][k], 4):
+            for a in range(4):
+                n_xv[k] = V(g.vector.tensor_scalar(block(T["et%d" % k], kk, a), block(T["en%d" % k], a, kk),
+                                                   T.fl[32 * a:32 * a + 32, 0:1], None, Op.max))
+
+    def v_c(k):
+        wait("v", "ss", n_xs[k])
+        for lo, hi in ((0, min(plan["by"][k], 2)), (2, plan["by"][k])):
+            if lo < hi:
+                n_xv[k] = carried = T["et%d" % k][32 * lo:32 * hi, :, :]
+                n_xv[k] = V(g.vector.tensor_scalar(carried, carried, T.fl[32 * lo:32 * hi, 0:1], None, Op.max))
+
+    def v_p(k):
+        wait("v", "vv", n_xv[k])
         P = T["p%d" % k]
-        wait("v", "vv", n_P[k])
         for b in range(4):
-            n = V(g.vector.transpose(P[:, b:512:4], et[:, b:512:4]))
-        wait("v", "vv", n)
+            n_P[k] = V(g.vector.transpose(P[:, b:512:4], T["et%d" % k][:, b, :]))
+        wait("v", "vv", n_P[k])
         n_pq[k] = V(g.vector.quantize_mx(words(T.pc, k), words(T.px, k), P[:]))
-        wait("y", "vv", n)
+        wait("y", "vv", n_P[k])
         g.sync.dma_start(T.p[order[k]], P[:]).then_inc(S.out, 16)
-        wait("t", "vv", n_pq[k])
-        out = bank(where(k, 1), lambda k=k: n_lt[k])
-        n_L[k] = M(g.tensor.matmul_mx(out, T.oc[:], T.ox[:], words(T.pc, k), words(T.px, k), True, True))
-        out = bank(where(k, 0), lambda k=k: n_ev[k])
-        n_A[k] = M(g.tensor.matmul_mx(out, T.vc[:], T.vx[:], words(T.pc, k), words(T.px, k), True, True))
 
-    def sums(k):
-        wait("v", "tt", n_L[k])
-        n_lt[k] = V(g.vector.transpose(words(T.lt, k), view(where(k, 1))))
-        wait("v", "tt", n_A[k])
-        n_ev[k] = V(g.vector.transpose(T["st%d" % k][:, 0:128], view(where(k, 0))))
-        wait("v", "vv", n_lt[k])
-        n_lc[k] = V(g.vector.tensor_copy(T["st%d" % k][:, 128:132], T.lt[:, 128 * k:128 * k + 128:32]))
-
-    def values(k):
+    def v_v(_k):
         wait("v", "lv", 16)
-        V(g.vector.quantize_mx(T.vc[:], T.vx[:], T.vt[:]))
+        n_v[0] = V(g.vector.quantize_mx(T.vc[:, 0:128], T.vx[:, 0:128], T.vt[:]))
 
-    def out_c(k):
-        n = V(g.vector.transpose(T.ct[0:32, 0:32], T.cn[0:32, 0:32]))
-        wait("v", "vv", n)
-        n = V(g.vector.tensor_scalar(T.cu[0:32, :], T.ct[0:32, :], -1.0, None, Op.mult))
-        wait("y", "vv", n)
-        g.sync.dma_start(T.c[:], T.cu[0:16, :]).then_inc(S.out, 16)
+    def t_A(k):
+        wait("t", "vv", max(n_pq[k], n_v[0]))
+        n_A[k] = M(g.tensor.matmul_mx(T.pa[:, 512 * k:512 * k + 256], words(T.pc, k), words(T.px, k), T.vc[:], T.vx[:],
+                                      True, True))
 
-    steps = {"S": scores, "h": shift, "c": clamp, "p": pack, "u": sums, "v": values, "C": out_c}
-    for s in plan["steps"].split():
-        steps[s[0]](int(s[1:] or 0))
+    def s_a(k):
+        wait("s", "tt", n_A[k])
+        n_a[k] = E(g.scalar.activation(T["st%d" % k][:], T.pa[:, 512 * k:512 * k + W], Fn.Copy))
+
+    steps = {"tS": t_S, "tA": t_A, "vr": v_r, "vx": v_x, "vc": v_c, "vp": v_p, "vv": v_v, "se": s_e, "sx": s_x, "sa": s_a}
+    needs = {"tS": [], "vv": [], "vr": ["tS"], "se": ["vr"], "sx": ["se"], "vx": ["se"], "vc": ["sx"], "vp": ["vx", "vc"],
+             "tA": ["vp", "vv"], "sa": ["tA"]}
+    todo = {q: plan[q].split() for q in "tvs"}
+    done = set()
+    while any(todo.values()):
+        left = sum(len(x) for x in todo.values())
+        for q in "tvs":
+            while todo[q]:
+                kind, k = q + todo[q][0][0], int(todo[q][0][1:] or 0)
+                if not all((d, 0 if d == "vv" else k) in done for d in needs[kind]):
+                    break
+                steps[kind](k)
+                done.add((kind, k))
+                todo[q].pop(0)
+        if left == sum(len(x) for x in todo.values()):
+            raise ValueError("the queues' orders wait for one another in a ring")
 
     def road(k, what):
         if k == PAR_:
-            return (cores[PAR],) + ((T.cpl[:], "cp") if what == "c" else (land(PAR, rank), "am%d" % rank))
+            return (cores[PAR],) + ((shift_of(rank), "cp") if what == "c" else (land(PAR, rank), "am%d" % rank))
         if is_gate:
             r = order[k]
-            return (cores[r],) + ((T.cyl[:, 0:4], "cyl") if what == "c" else (land(r, rank), "am%d" % rank))
+            return (cores[r],) + ((shift_of(rank), "cyl") if what == "c" else (land(r, rank), "am%d" % rank))
         if what == "c":
-            return (helper,) + ((T.fc[:, 0:4], "rcx") if k == X_ else (T.fc[:, 4:8], "rcy"))
+            return (helper,) + ((T.fc[:, 0:1], "rcx") if k == X_ else (T.fc[:, 4:5], "rcy"))
         return (helper,) + ((T.fx[:], "rx") if k == X_ else (T.fy[:], "ry"))
 
-    for s in plan["sends"]:
+    for s in plan["sends"].split():
         k = int(s[1])
-        wait("g", "vv", n_neg[k] if s[0] == "c" else max(n_lc[k], n_ev[k]))
+        wait("g", "ss", n_c[k] if s[0] == "c" else n_a[k])
         send(cneg(k) if s[0] == "c" else T["st%d" % k][:], *road(k, s[0]))
 
-    def tiny(j):
-        return T.tiny[:, 4 * j:4 * j + 4]
-
+    wait("v", "ss", max(n_c.values()))
+    V(g.vector.tensor_scalar(T.cw[:, 0:4], T.cn[:, 0:4], -1.0, None, Op.mult))
+    n = V(g.vector.tensor_copy(shift_of(rank), cneg(OWN_)))
     wait("v", "cp", ne)
     wait("v", "cyl", 2 * ne)
-    neg = {rank: cneg(OWN_), PAR: T.cpl[:], FG: T.cyl[:, 0:4], FN: T.cyl[:, 4:8]}
-    V(g.vector.tensor_tensor(tiny(0), neg[rank], neg[PAR], Op.min))
-    n = V(g.vector.tensor_tensor(tiny(1), neg[FG], neg[FN], Op.min))
     wait("v", "vv", n)
-    n = V(g.vector.tensor_tensor(tiny(2), tiny(0), tiny(1), Op.min))
-    wait("v", "vv", n)
-    for j in order:
-        n = V(g.vector.tensor_tensor(T.dd[:, 4 * j:4 * j + 4], tiny(2), neg[j], Op.subtract))
+    n = V(g.vector.tensor_reduce(T.mn[:, 0:1], T.cl[:, 0:16:4], AX, Op.min))
     wait("s", "vv", n)
-    nx = E(g.scalar.activation(T.ww[:, 0:16], T.dd[:], Fn.Exp))
+    nx = E(g.scalar.activation(T.cw[:, 4:8], T.cl[:, 0:16:4], Fn.Exp, bias=T.mn[:, 0:1], scale=-1.0))
+    wait("v", "ss", nx)
+    n = V(g.vector.transpose(T.cwt[:], T.cw[:]))
+    wait("y", "vv", n)
+    for a in range(4):
+        g.sync.dma_start(T.c[:, 32 * a:32 * a + 32], T.cwt[32 * a:32 * a + 4, :]).then_inc(S.out, 16)
+        g.sync.dma_start(T.w[:, 32 * a:32 * a + 32], T.cwt[32 * a + 4:32 * a + 8, :]).then_inc(S.out, 16)
 
-    src = {rank: T.st0, PAR: T.al1, FG: T.al2, FN: T.al3}
-    arrive = [rank, FG, FN, PAR] if is_gate else [rank, PAR, FG, FN]
-    den, acc, nn = None, None, 0
-    for j, r in enumerate(arrive):
-        last = j == len(arrive) - 1
-        if j == 0:
+    arrive = [OWN_, X_, Y_, PAR_] if is_gate else [OWN_, PAR_, X_, Y_]
+    acc = None
+    for j, k in enumerate(arrive):
+        r = order[k]
+        if k == OWN_:
             wait("s", "ss", nx)
+            wait("s", "tt", n_A[k])
+            src = T.pa[:, 512 * k:512 * k + W]
         else:
             wait("s", "am%d" % r, ne)
-        for b in range(4):
-            c = 256 * j + 32 * b
-            ns = E(g.scalar.activation(T.num[:, c:c + 32], src[r][:, 32 * b:32 * b + 32], Fn.Copy,
-                                       scale=T.ww[:, 4 * r + b:4 * r + b + 1]))
+            src = T["al%d" % k][:]
+        nu = T["nu%d" % j]
+        ns = E(g.scalar.activation(nu[:], src, Fn.Copy, scale=T.cw[:, 4 + r:5 + r]))
         if j == 0:
-            wait("v", "ss", nx)
-            n = V(g.vector.transpose(T.wt[0:32, 0:32], T.ww[0:32, 0:32]))
-            wait("y", "vv", n)
-            g.sync.dma_start(T.w[:], T.wt[0:16, :]).then_inc(S.out, 16)
-        else:
-            wait("v", "am%d" % r, ne)
-        nd = V(g.vector.tensor_tensor(tiny(4 + 2 * j), src[r][:, 128:132], T.ww[:, 4 * r:4 * r + 4], Op.mult))
-        if j == 0:
-            den, acc = tiny(4), words(T.num, 0)
+            acc = nu
             continue
-        wait("v", "vv", nd)
-        nd = V(g.vector.tensor_tensor(tiny(5 + 2 * j), den, tiny(4 + 2 * j), Op.add))
-        den = tiny(5 + 2 * j)
-        if last:
-            wait("v", "vv", nd)
-            nd = V(g.vector.reciprocal(tiny(3), den))
         wait("v", "ss", ns)
-        wait("v", "vv", nn)
-        nn = V(g.vector.tensor_tensor(words(T.num, 2 * j + 1), acc, words(T.num, 2 * j), Op.add))
-        acc = words(T.num, 2 * j + 1)
-    wait("v", "vv", max(nd, nn))
-    o = 128 * (2 * len(arrive) - 1)
-    for b in range(4):
-        n = V(g.vector.tensor_scalar(T.rt[:, 32 * b:32 * b + 32], T.num[:, o + 32 * b:o + 32 * b + 32],
-                                     T.tiny[:, 12 + b:13 + b], None, Op.mult))
+        if j > 1:
+            wait("v", "vv", n)
+        n = V(g.vector.tensor_tensor(T["ac%d" % j][:], acc[:], nu[:], Op.add))
+        acc = T["ac%d" % j]
+    wait("v", "vv", n)
+    n = V(g.vector.reciprocal(T.ri[:, 0:1], acc[:, 128:129]))
+    wait("s", "vv", n)
+    wait("v", "vv", n)
+    for a in range(4):
+        for d in range(4):
+            out, src = T.rt[32 * d:32 * d + 32, 32 * a:32 * a + 32], acc[32 * a:32 * a + 32, 32 * d:32 * d + 32]
+            by = T.ri[32 * a:32 * a + 32, 0:1]
+            if a % 2:
+                ns = E(g.scalar.activation(out, src, Fn.Copy, scale=by))
+            else:
+                n = V(g.vector.tensor_scalar(out, src, by, None, Op.mult))
+    wait("v", "ss", ns)
     wait("v", "vv", n)
     n = V(g.vector.transpose(T.res[:], T.rt[:]))
     wait("y", "vv", n)
     g.sync.dma_start(T.o[:], T.res[:]).then_inc(S.out, 16)
-    g.sync.wait_ge(S.out, 16 * 7)
+    g.sync.wait_ge(S.out, 16 * 13)
     wait("g", "ss", tick["ss"])
     wait("g", "tt", tick["tt"])
     wait("g", "ls", sent[0])

@@ -17,7 +17,8 @@ SCRATCH = {
     "m20": ("sbuf", [128, 8], F), "fl": ("sbuf", [128, 8], B),
     "rm": ("sbuf", [128, 16], F), "cn": ("sbuf", [128, 16], F),
     "cw": ("sbuf", [128, 32], F), "cwt": ("sbuf", [128, 32], F),
-    "cl": ("sbuf", [128, 16], F), "mn": ("sbuf", [128, 4], F), "ri": ("sbuf", [128, 4], F),
+    "cl": ("sbuf", [128, 16], F), "mn": ("sbuf", [128, 4], F),
+    "dn": ("sbuf", [128, 4], F), "ri": ("sbuf", [128, 4], F),
     "fx": ("sbuf", [128, W], F), "fy": ("sbuf", [128, W], F), "fc": ("sbuf", [128, 8], F),
     "rt": ("sbuf", [128, 128], F), "res": ("sbuf", [128, 128], F),
     "ps": ("psum", [128, 2048], F), "pa": ("psum", [128, 2048], F),
@@ -37,21 +38,22 @@ SEMAPHORES = (["vv", "tt", "ss", "lq", "lv", "out", "rx", "ry", "rcx", "rcy", "c
 SCALE = float(np.float32(0.0125))
 
 PLAN_GATE = {
-    "t": "S0 S1 S2 S3 A1 A2 A3 A0",
-    "v": "r0 x0 r1 c0 v r2 c1 p0 x1 p1 r3 c2 x2 p2 x3 c3 p3",
-    "s": "e0 x0 e1 x1 e2 x2 e3 a1 x3 a2 a3",
-    "q": "FN FG PAR RFN RFG",
-    "by": [1, 2, 3, 2],
-    "sends": "c2 c1 A1 A2 c3 A3",
+    "t": "S0 S1 S2 S3 A2 A3 A1 A0",
+    "v": "r0 n0 x0:1 x0:3 r2 r1 v x2:3 x2:2 x2:1 r3 x2:0 n3 x1:2 x1:3 p2 x3:1 x3:3 x3:2 x3:0 p3 c1 p1 W c0 x0:2 h2 p0 U h0 h3 h1",
+    "s": "n0 e0 n2 e2 n1 e1 x1:1 x0:0 e3 a2 x1:0 a3 a1 w h3 h2 h0 h1".replace("n0 ", ""),
+    "y": "P0 P1 P2 U P3",
+    "sends": "c3 c2 c1 A2 A3 A1",
+    "q": "FN FG *FN *FG PAR",
 }
 PLAN_NEIGHBOUR = {
-    "t": "S0 S2 S1 S3 A0 A2 A3 A1",
-    "v": "r0 r2 c0 x0 p0 x2 v r3 r1 c2 p2 x3 c3 p3 x1 c1 p1",
-    "s": "e0 x0 e2 x2 e3 x3 e1 a2 x1 a3 a1",
+    "t": "S0 S2 S3 S1 A2 A0 A3 A1",
+    "v": "v r0 n0 x0:2 r2 x0:1 c0 x0:3 p0 r3 x2:1 x2:3 c2 x2:2 x3:2 p2 r1 x3:3 c3 p3 x1:0 x1:3 x1:1 W x1:2 p1 U h1 h0 h2 h3",
+    "s": "e0 x0:0 n2 e2 x2:0 n3 e3 x3:0 x3:1 a2 n1 e1 a3 w a1 h0 h1 h2 h3",
+    "y": "P0 P2 P3 P1 U",
+    "sends": "c2 c3 A2 c1 A3 A1",
     "q": "PAR",
-    "by": [3, 1, 1, 1],
-    "sends": "c2 c3 c1 A2 A3 A1",
 }
+TAIL_SCALAR = 5
 
 
 def rank_program(g, core, T, topo):
@@ -127,6 +129,9 @@ def rank_program(g, core, T, topo):
     def shift_of(r):
         return T.cl[:, 4 * r:4 * r + 1]
 
+    def words(buf, k):
+        return buf[:, 128 * k:128 * k + 128]
+
     if rank is None:
         for sem, src, to, dst, arrive in (
                 ("rcx", T.fc[:, 0:1], FG, shift_of(nbr), "cyl"), ("rcy", T.fc[:, 4:5], FN, shift_of(nbr), "cyl"),
@@ -146,33 +151,36 @@ def rank_program(g, core, T, topo):
     V(g.vector.memset(T.cw[:, 8:32], 0.0))
     wait("s", "vv", n_m20)
     n_fl = E(g.scalar.activation(T.fl[:], T.m20[:], Fn.Exp))
-    wait("v", "lq", 16)
-    n_q = V(g.vector.quantize_mx(T.qc[:, 0:128], T.qx[:, 0:128], T.qt[:]))
     wait("v", "vv", n_ot)
     V(g.vector.quantize_mx(T.vc[:, 128:256], T.vx[:, 128:256], T.ot[:]))
+    wait("v", "lq", 16)
+    n_q = V(g.vector.quantize_mx(words(T.qc, OWN_), words(T.qx, OWN_), T.qt[:]))
 
     def send_q(s, r):
-        i, o = 128 * slot_at(rank, s), 128 * slot_at(r, s)
+        i, o = slot_at(rank, s), slot_at(r, s)
         if s != rank:
             wait("g", "qa%d" % s, ne)
-        send(T.qc[:, i:i + 128].bitcast(dt.uint8), cores[r], T.qc[:, o:o + 128].bitcast(dt.uint8), "qa%d" % s)
+        send(words(T.qc, i).bitcast(dt.uint8), cores[r], words(T.qc, o).bitcast(dt.uint8), "qa%d" % s)
         if s != rank:
             wait("g", "qb%d" % s, ne)
-        send(T.qx[:, i:i + 128], cores[r], T.qx[:, o:o + 128], "qb%d" % s)
+        send(words(T.qx, i), cores[r], words(T.qx, o), "qb%d" % s)
 
     wait("g", "vv", n_q)
     for step in plan["q"].split():
-        send_q(*{"FN": (rank, FN), "FG": (rank, FG), "PAR": (rank, PAR), "RFN": (PAR, FN), "RFG": (PAR, FG)}[step])
+        send_q(PAR if step[0] == "*" else rank, {"FN": FN, "FG": FG, "PAR": PAR}[step.strip("*")])
 
     for h in range(4):
         wait("v", "lk%d" % h, 16)
-        n_k = V(g.vector.quantize_mx(T.kc[:, 128 * h:128 * h + 128], T.kx[:, 128 * h:128 * h + 128],
-                                     T.kt[:, 512 * h:512 * h + 512]))
+        n_k = V(g.vector.quantize_mx(words(T.kc, h), words(T.kx, h), T.kt[:, 512 * h:512 * h + 512]))
 
-    n_S, n_A, n_r, n_c, n_e, n_xs, n_xv, n_P, n_pq, n_a, n_v = {}, {}, {}, {}, {}, {}, {}, {}, {}, {}, {}
+    n_S, n_A, n_r, n_c, n_e, n_xs, n_xv, n_P, n_pq, n_a, n_v, n_h, n_t = ({} for _ in range(13))
+    acc = {"adds": 0}
 
-    def words(buf, k):
-        return buf[:, 128 * k:128 * k + 128]
+    def on(k):
+        return "v" if "n%s" % k in plan["v"].split() else "s"
+
+    def groups(q, k):
+        return sorted(int(t[3:]) for t in plan[q].split() if t[:2] == "x%s" % k)
 
     def scores(k):
         return T.ps[:, 512 * k:512 * k + 512]
@@ -191,33 +199,38 @@ def rank_program(g, core, T, topo):
     def cneg(k):
         return T.cn[:, order[k]:order[k] + 1]
 
-    def s_e(k):
+    def v_n(k):
+        wait("v", "vv", n_r[k])
+        n_c[k] = ("vv", V(g.vector.tensor_scalar(cneg(k), T.rm[:, k:k + 1], SCALE, None, Op.mult)))
+
+    def s_n(k):
         wait("s", "vv", n_r[k])
-        n_c[k] = E(g.scalar.activation(cneg(k), T.rm[:, k:k + 1], Fn.Copy, scale=SCALE))
-        wait("s", "ss", n_c[k])
+        n_c[k] = ("ss", E(g.scalar.activation(cneg(k), T.rm[:, k:k + 1], Fn.Copy, scale=SCALE)))
+
+    def s_e(k):
+        wait("s", *n_c[k])
         n_e[k] = E(g.scalar.activation(T["en%d" % k][:, :, :], scores(k), Fn.Exp, bias=cneg(k), scale=SCALE))
 
     def block(buf, part, col):
         return buf[32 * part:32 * part + 32, :, 32 * col:32 * col + 32]
 
-    def s_x(k):
+    def s_x(k, kk):
         wait("s", "ss", n_e[k])
-        for kk in range(plan["by"][k]):
-            for a in range(4):
-                n_xs[k] = E(g.scalar.activation(block(T["et%d" % k], kk, a), block(T["en%d" % k], a, kk), Fn.Copy))
+        for a in range(4):
+            n_xs[k] = E(g.scalar.activation(block(T["et%d" % k], kk, a), block(T["en%d" % k], a, kk), Fn.Copy))
 
-    def v_x(k):
-        wait("v", "ss", n_e[k])
-        for kk in range(plan["by"][k], 4):
-            for a in range(4):
-                n_xv[k] = V(g.vector.tensor_scalar(block(T["et%d" % k], kk, a), block(T["en%d" % k], a, kk),
-                                                   T.fl[32 * a:32 * a + 32, 0:1], None, Op.max))
+    def v_x(k, kk):
+        wait("v", "ss", max(n_fl, n_e[k]))
+        for a in range(4):
+            n_xv[k] = V(g.vector.tensor_scalar(block(T["et%d" % k], kk, a), block(T["en%d" % k], a, kk),
+                                               T.fl[32 * a:32 * a + 32, 0:1], None, Op.max))
 
     def v_c(k):
         wait("v", "ss", n_xs[k])
-        for lo, hi in ((0, min(plan["by"][k], 2)), (2, plan["by"][k])):
+        n = len(groups("s", k))
+        for lo, hi in ((0, min(n, 2)), (2, n)):
             if lo < hi:
-                n_xv[k] = carried = T["et%d" % k][32 * lo:32 * hi, :, :]
+                carried = T["et%d" % k][32 * lo:32 * hi, :, :]
                 n_xv[k] = V(g.vector.tensor_scalar(carried, carried, T.fl[32 * lo:32 * hi, 0:1], None, Op.max))
 
     def v_p(k):
@@ -227,12 +240,14 @@ def rank_program(g, core, T, topo):
             n_P[k] = V(g.vector.transpose(P[:, b:512:4], T["et%d" % k][:, b, :]))
         wait("v", "vv", n_P[k])
         n_pq[k] = V(g.vector.quantize_mx(words(T.pc, k), words(T.px, k), P[:]))
+
+    def y_P(k):
         wait("y", "vv", n_P[k])
-        g.sync.dma_start(T.p[order[k]], P[:]).then_inc(S.out, 16)
+        g.sync.dma_start(T.p[order[k]], T["p%d" % k][:]).then_inc(S.out, 16)
 
     def v_v(_k):
         wait("v", "lv", 16)
-        n_v[0] = V(g.vector.quantize_mx(T.vc[:, 0:128], T.vx[:, 0:128], T.vt[:]))
+        n_v[0] = V(g.vector.quantize_mx(words(T.vc, 0), words(T.vx, 0), T.vt[:]))
 
     def t_A(k):
         wait("t", "vv", max(n_pq[k], n_v[0]))
@@ -243,20 +258,96 @@ def rank_program(g, core, T, topo):
         wait("s", "tt", n_A[k])
         n_a[k] = E(g.scalar.activation(T["st%d" % k][:], T.pa[:, 512 * k:512 * k + W], Fn.Copy))
 
-    steps = {"tS": t_S, "tA": t_A, "vr": v_r, "vx": v_x, "vc": v_c, "vp": v_p, "vv": v_v, "se": s_e, "sx": s_x, "sa": s_a}
-    needs = {"tS": [], "vv": [], "vr": ["tS"], "se": ["vr"], "sx": ["se"], "vx": ["se"], "vc": ["sx"], "vp": ["vx", "vc"],
-             "tA": ["vp", "vv"], "sa": ["tA"]}
-    todo = {q: plan[q].split() for q in "tvs"}
+    def v_W(_k):
+        wait("v", *n_c[OWN_])
+        n = V(g.vector.tensor_copy(shift_of(rank), cneg(OWN_)))
+        wait("v", "cp", ne)
+        wait("v", "cyl", 2 * ne)
+        wait("v", "vv", n)
+        n_t["W"] = V(g.vector.tensor_reduce(T.mn[:, 0:1], T.cl[:, 0:16:4], AX, Op.min))
+
+    def s_w(_k):
+        wait("s", "vv", n_t["W"])
+        n_t["w"] = E(g.scalar.activation(T.cw[:, 4:8], T.cl[:, 0:16:4], Fn.Exp, bias=T.mn[:, 0:1], scale=-1.0))
+
+    def v_U(_k):
+        for k in range(4):
+            wait("v", *n_c[k])
+        n = V(g.vector.tensor_scalar(T.cw[:, 0:4], T.cn[:, 0:4], -1.0, None, Op.mult))
+        wait("v", "ss", n_t["w"])
+        wait("v", "vv", n)
+        n_t["U"] = V(g.vector.transpose(T.cwt[:], T.cw[:]))
+
+    def y_U(_k):
+        wait("y", "vv", n_t["U"])
+        for a in range(4):
+            g.sync.dma_start(T.c[:, 32 * a:32 * a + 32], T.cwt[32 * a:32 * a + 4, :]).then_inc(S.out, 16)
+            g.sync.dma_start(T.w[:, 32 * a:32 * a + 32], T.cwt[32 * a + 4:32 * a + 8, :]).then_inc(S.out, 16)
+
+    last = [int(t[1]) for t in plan["v"].split() if t[0] == "h"][-1]
+
+    def weight(k):
+        return T.cw[:, 4 + order[k]:5 + order[k]]
+
+    def width(k):
+        return 128 if k == last else W
+
+    def s_h(k):
+        wait("s", "ss", n_t["w"])
+        if k == OWN_:
+            wait("s", "tt", n_A[k])
+            src = T.pa[:, 512 * k:512 * k + width(k)]
+        else:
+            wait("s", "am%d" % order[k], ne)
+            src = T["al%d" % k][:, 0:width(k)]
+        n_h[k] = E(g.scalar.activation(T["nu%d" % k][:, 0:width(k)], src, Fn.Copy, scale=weight(k)))
+
+    def v_h(k):
+        if "at" not in acc:
+            acc["at"], acc["n"] = T["nu%d" % k], ("ss", n_h[k])
+            return
+        if k == last:
+            wait("v", "ss", n_t["w"])
+            wait("v", "am%d" % order[k], ne)
+            wait("v", *acc["n"])
+            n = V(g.vector.tensor_scalar(T.dn[:, 0:1], T["al%d" % k][:, 128:129], weight(k), acc["at"][:, 128:129],
+                                         Op.mult, Op.add))
+            wait("v", "vv", n)
+            V(g.vector.reciprocal(T.ri[:, 0:1], T.dn[:, 0:1]))
+        wait("v", *acc["n"])
+        wait("v", "ss", n_h[k])
+        acc["adds"] += 1
+        to, n = T["ac%d" % acc["adds"]], width(k)
+        acc["n"] = ("vv", V(g.vector.tensor_tensor(to[:, 0:n], acc["at"][:, 0:n], T["nu%d" % k][:, 0:n], Op.add)))
+        acc["at"] = to
+
+    steps = {"tS": t_S, "tA": t_A, "vr": v_r, "vn": v_n, "sn": s_n, "vx": v_x, "vc": v_c, "vp": v_p, "vv": v_v, "se": s_e,
+             "sx": s_x, "sa": s_a, "vW": v_W, "sw": s_w, "vU": v_U, "sh": s_h, "vh": v_h, "yP": y_P, "yU": y_U}
+
+    def needs(q, t):
+        kind, k = q + t[0], t[1:2]
+        if kind == "vc":
+            return ["sx%s:%d" % (k, x) for x in groups("s", k)]
+        if kind == "vp":
+            return ["vx%s:%d" % (k, x) for x in groups("v", k)] + (["vc" + k] if groups("s", k) else [])
+        if kind == "vU":
+            return ["sw"] + [on(j) + "n%d" % j for j in range(4)]
+        return {"tS": [], "vv": [], "vr": ["tS" + k], "vn": ["vr" + k], "sn": ["vr" + k], "se": [on(k) + "n" + k],
+                "sx": ["se" + k], "vx": ["se" + k], "tA": ["vp" + k, "vv"], "sa": ["tA" + k], "vW": [on(OWN_) + "n0"],
+                "sw": ["vW"], "sh": ["sw"] + (["tA0"] if k == "0" else []), "vh": ["sh" + k], "yP": ["vp" + k],
+                "yU": ["vU"]}[kind]
+
+    todo = {q: plan[q].split() for q in "tvsy"}
     done = set()
     while any(todo.values()):
         left = sum(len(x) for x in todo.values())
-        for q in "tvs":
+        for q in "tvsy":
             while todo[q]:
-                kind, k = q + todo[q][0][0], int(todo[q][0][1:] or 0)
-                if not all((d, 0 if d == "vv" else k) in done for d in needs[kind]):
+                t = todo[q][0]
+                if not all(d in done for d in needs(q, t)):
                     break
-                steps[kind](k)
-                done.add((kind, k))
+                steps[q + t[0]](*([int(x) for x in t[1:].split(":")] if t[1:] else [0]))
+                done.add(q + t)
                 todo[q].pop(0)
         if left == sum(len(x) for x in todo.values()):
             raise ValueError("the queues' orders wait for one another in a ring")
@@ -273,58 +364,23 @@ def rank_program(g, core, T, topo):
 
     for s in plan["sends"].split():
         k = int(s[1])
-        wait("g", "ss", n_c[k] if s[0] == "c" else n_a[k])
-        send(cneg(k) if s[0] == "c" else T["st%d" % k][:], *road(k, s[0]))
-
-    wait("v", "ss", max(n_c.values()))
-    V(g.vector.tensor_scalar(T.cw[:, 0:4], T.cn[:, 0:4], -1.0, None, Op.mult))
-    n = V(g.vector.tensor_copy(shift_of(rank), cneg(OWN_)))
-    wait("v", "cp", ne)
-    wait("v", "cyl", 2 * ne)
-    wait("v", "vv", n)
-    n = V(g.vector.tensor_reduce(T.mn[:, 0:1], T.cl[:, 0:16:4], AX, Op.min))
-    wait("s", "vv", n)
-    nx = E(g.scalar.activation(T.cw[:, 4:8], T.cl[:, 0:16:4], Fn.Exp, bias=T.mn[:, 0:1], scale=-1.0))
-    wait("v", "ss", nx)
-    n = V(g.vector.transpose(T.cwt[:], T.cw[:]))
-    wait("y", "vv", n)
-    for a in range(4):
-        g.sync.dma_start(T.c[:, 32 * a:32 * a + 32], T.cwt[32 * a:32 * a + 4, :]).then_inc(S.out, 16)
-        g.sync.dma_start(T.w[:, 32 * a:32 * a + 32], T.cwt[32 * a + 4:32 * a + 8, :]).then_inc(S.out, 16)
-
-    arrive = [OWN_, X_, Y_, PAR_] if is_gate else [OWN_, PAR_, X_, Y_]
-    acc = None
-    for j, k in enumerate(arrive):
-        r = order[k]
-        if k == OWN_:
-            wait("s", "ss", nx)
-            wait("s", "tt", n_A[k])
-            src = T.pa[:, 512 * k:512 * k + W]
+        if s[0] == "c":
+            wait("g", *n_c[k])
+            send(cneg(k), *road(k, "c"))
         else:
-            wait("s", "am%d" % r, ne)
-            src = T["al%d" % k][:]
-        nu = T["nu%d" % j]
-        ns = E(g.scalar.activation(nu[:], src, Fn.Copy, scale=T.cw[:, 4 + r:5 + r]))
-        if j == 0:
-            acc = nu
-            continue
-        wait("v", "ss", ns)
-        if j > 1:
-            wait("v", "vv", n)
-        n = V(g.vector.tensor_tensor(T["ac%d" % j][:], acc[:], nu[:], Op.add))
-        acc = T["ac%d" % j]
-    wait("v", "vv", n)
-    n = V(g.vector.reciprocal(T.ri[:, 0:1], acc[:, 128:129]))
-    wait("s", "vv", n)
-    wait("v", "vv", n)
-    for a in range(4):
-        for d in range(4):
-            out, src = T.rt[32 * d:32 * d + 32, 32 * a:32 * a + 32], acc[32 * a:32 * a + 32, 32 * d:32 * d + 32]
-            by = T.ri[32 * a:32 * a + 32, 0:1]
-            if a % 2:
-                ns = E(g.scalar.activation(out, src, Fn.Copy, scale=by))
-            else:
-                n = V(g.vector.tensor_scalar(out, src, by, None, Op.mult))
+            wait("g", "ss", n_a[k])
+            send(T["st%d" % k][:], *road(k, "A"))
+
+    wait("s", *acc["n"])
+    wait("v", *acc["n"])
+    for i in range(16):
+        a, d = i // 4, i % 4
+        out, src = T.rt[32 * d:32 * d + 32, 32 * a:32 * a + 32], acc["at"][32 * a:32 * a + 32, 32 * d:32 * d + 32]
+        by = T.ri[32 * a:32 * a + 32, 0:1]
+        if i < TAIL_SCALAR:
+            ns = E(g.scalar.activation(out, src, Fn.Copy, scale=by))
+        else:
+            n = V(g.vector.tensor_scalar(out, src, by, None, Op.mult))
     wait("v", "ss", ns)
     wait("v", "vv", n)
     n = V(g.vector.transpose(T.res[:], T.rt[:]))

import numpy as np
from concourse.bass import DstId, RemoteDMATransfer
from concourse.mybir import dt, AluOpType, AxisListType, ActivationFunctionType

F = "float32"
B = "bfloat16"
C4 = "float8_e4m3fn_x4"
U8 = "uint8"
W = 129
SCRATCH = {
    "qt": ("sbuf", [128, 512], B), "kt": ("sbuf", [128, 2048], B), "vt": ("sbuf", [128, 512], B),
    "ot": ("sbuf", [128, 512], B),
    "qc": ("sbuf", [128, 512], C4), "qx": ("sbuf", [128, 512], U8),
    "kc": ("sbuf", [128, 512], C4), "kx": ("sbuf", [128, 512], U8),
    "vc": ("sbuf", [128, 256], C4), "vx": ("sbuf", [128, 256], U8),
    "pc": ("sbuf", [128, 512], C4), "px": ("sbuf", [128, 512], U8),
    "m20": ("sbuf", [128, 8], F), "fl": ("sbuf", [128, 8], B),
    "rm": ("sbuf", [128, 16], F), "cn": ("sbuf", [128, 16], F),
    "cw": ("sbuf", [128, 32], F), "cwt": ("sbuf", [128, 32], F),
    "cl": ("sbuf", [128, 16], F), "mn": ("sbuf", [128, 4], F),
    "dn": ("sbuf", [128, 4], F), "ri": ("sbuf", [128, 4], F),
    "fx": ("sbuf", [128, W], F), "fy": ("sbuf", [128, W], F), "fc": ("sbuf", [128, 8], F),
    "rt": ("sbuf", [128, 128], F), "res": ("sbuf", [128, 128], F),
    "ps": ("psum", [128, 2048], F), "pa": ("psum", [128, 2048], F),
}
for _k in range(4):
    SCRATCH["en%d" % _k] = ("sbuf", [128, 4, 128], B)
    SCRATCH["et%d" % _k] = ("sbuf", [128, 4, 128], B)
    SCRATCH["p%d" % _k] = ("sbuf", [128, 512], B)
    SCRATCH["nu%d" % _k] = ("sbuf", [128, W], F)
    if _k:
        SCRATCH["st%d" % _k] = ("sbuf", [128, W], F)
        SCRATCH["al%d" % _k] = ("sbuf", [128, W], F)
        SCRATCH["ac%d" % _k] = ("sbuf", [128, W], F)
SEMAPHORES = (["vv", "tt", "ss", "lq", "lv", "out", "rx", "ry", "rcx", "rcy", "cp", "cyl", "ls"]
              + [s + "%d" % r for s in ("lk", "qa", "qb", "am") for r in range(4)])

SCALE = float(np.float32(0.0125))

PLAN_GATE = {
    "t": "S0 S1 S2 S3 A2 A3 A1 A0",
    "v": "r0 n0 x0:1 x0:3 r2 r1 v x2:3 x2:2 x2:1 r3 x2:0 n3 x1:2 x1:3 p2 x3:1 x3:3 x3:2 x3:0 p3 c1 p1 W c0 x0:2 h2 p0 U h0 h3 h1",
    "s": "n0 e0 n2 e2 n1 e1 x1:1 x0:0 e3 a2 x1:0 a3 a1 w h3 h2 h0 h1".replace("n0 ", ""),
    "y": "P0 P1 P2 U P3",
    "sends": "c3 c2 c1 A2 A3 A1",
    "q": "FN FG *FN *FG PAR",
}
PLAN_NEIGHBOUR = {
    "t": "S0 S2 S3 S1 A2 A0 A3 A1",
    "v": "v r0 n0 x0:2 r2 x0:1 c0 x0:3 p0 r3 x2:1 x2:3 c2 x2:2 x3:2 p2 r1 x3:3 c3 p3 x1:0 x1:3 x1:1 W x1:2 p1 U h1 h0 h2 h3",
    "s": "e0 x0:0 n2 e2 x2:0 n3 e3 x3:0 x3:1 a2 n1 e1 a3 w a1 h0 h1 h2 h3",
    "y": "P0 P2 P3 P1 U",
    "sends": "c2 c3 A2 c1 A3 A1",
    "q": "PAR",
}
TAIL_SCALAR = 5


def rank_program(g, core, T, topo):
    S = T.sem
    cores = T.cores
    n_ranks = len(cores)
    rank = T.rank_of(core)
    if all(topo.chip(core) != topo.chip(c) for c in cores):
        return
    Op, Fn, AX = AluOpType, ActivationFunctionType, AxisListType.X

    def gate_of(c):
        mine = [r for r in range(n_ranks) if topo.chip(cores[r]) == topo.chip(c)]
        away = [r for r in range(n_ranks) if r not in mine]
        ok = [r for r in mine if all(topo.may_write(cores[r], cores[a]) for a in away)]
        return ok[0], [r for r in mine if r != ok[0]][0], away

    def order_of(r):
        ga, nb, away = gate_of(cores[r])
        fg, fn, _ = gate_of(cores[away[0]])
        return [r, nb if r == ga else ga, fg, fn]

    gate, nbr, away = gate_of(core)
    helper = [c for c in range(topo.CHIPS * topo.CORES_PER_CHIP) if topo.chip(c) == topo.chip(core) and c not in cores
              and topo.die(c) == topo.die(cores[nbr]) and all(topo.may_write(c, cores[r]) for r in away)][0]
    if rank is None and core != helper:
        return
    is_gate = rank == gate
    plan = PLAN_GATE if is_gate else PLAN_NEIGHBOUR
    order = order_of(nbr if rank is None else rank)
    _, PAR, FG, FN = order
    OWN_, PAR_, X_, Y_ = 0, 1, 2, 3
    lanes = topo.mask(core, cores[FG])
    ne = bin(lanes).count("1")

    queues = {"v": g.vector, "t": g.tensor, "s": g.scalar, "y": g.sync, "g": g}
    tick = {"vv": 0, "tt": 0, "ss": 0}
    seen = {}

    def wait(q, sem, n):
        if n > 0 and seen.get((q, sem), 0) < n:
            queues[q].wait_ge(T.sem[sem], n)
            seen[(q, sem)] = n

    def mark(ins, sem):
        ins.then_inc(T.sem[sem], 1)
        tick[sem] += 1
        return tick[sem]

    def V(ins):
        return mark(ins, "vv")

    def E(ins):
        return mark(ins, "ss")

    def M(ins):
        return mark(ins, "tt")

    sent = [0]

    def send(src, dst_core, dst, sem):
        rid, pid, _s = topo.addr(dst_core)
        g.remote_dma_fused([RemoteDMATransfer(dst_ids=[DstId(rid=rid, pnc=pid)], dma_engine_mask=lanes,
                                              remote_sem=T.sem[sem], srcs=[src], dsts=[dst])], local_sem=T.sem["ls"])
        sent[0] += ne

    def slot_at(r, s):
        return order_of(r).index(s)

    def land(r, s):
        return T["al%d" % slot_at(r, s)][:]

    def shift_of(r):
        return T.cl[:, 4 * r:4 * r + 1]

    def words(buf, k):
        return buf[:, 128 * k:128 * k + 128]

    if rank is None:
        for sem, src, to, dst, arrive in (
                ("rcx", T.fc[:, 0:1], FG, shift_of(nbr), "cyl"), ("rcy", T.fc[:, 4:5], FN, shift_of(nbr), "cyl"),
                ("rx", T.fx[:], FG, land(FG, nbr), "am%d" % nbr), ("ry", T.fy[:], FN, land(FN, nbr), "am%d" % nbr)):
            wait("g", sem, ne)
            send(src, cores[to], dst, arrive)
        wait("g", "ls", sent[0])
        return

    g.sync.dma_start(T.qt[:], T.q[:]).then_inc(S.lq, 16)
    for h in range(4):
        g.sync.dma_start(T.kt[:, 512 * h:512 * h + 512], T.k[:, 512 * h:512 * h + 512]).then_inc(T.sem["lk%d" % h], 16)
    g.sync.dma_start(T.vt[:], T.v[:]).then_inc(S.lv, 16)

    n_m20 = V(g.vector.memset(T.m20[:], -20.0))
    n_ot = V(g.vector.memset(T.ot[:], 1.0))
    V(g.vector.memset(T.cw[:, 8:32], 0.0))
    wait("s", "vv", n_m20)
    n_fl = E(g.scalar.activation(T.fl[:], T.m20[:], Fn.Exp))
    wait("v", "vv", n_ot)
    V(g.vector.quantize_mx(T.vc[:, 128:256], T.vx[:, 128:256], T.ot[:]))
    wait("v", "lq", 16)
    n_q = V(g.vector.quantize_mx(words(T.qc, OWN_), words(T.qx, OWN_), T.qt[:]))

    def send_q(s, r):
        i, o = slot_at(rank, s), slot_at(r, s)
        if s != rank:
            wait("g", "qa%d" % s, ne)
        send(words(T.qc, i).bitcast(dt.uint8), cores[r], words(T.qc, o).bitcast(dt.uint8), "qa%d" % s)
        if s != rank:
            wait("g", "qb%d" % s, ne)
        send(words(T.qx, i), cores[r], words(T.qx, o), "qb%d" % s)

    wait("g", "vv", n_q)
    for step in plan["q"].split():
        send_q(PAR if step[0] == "*" else rank, {"FN": FN, "FG": FG, "PAR": PAR}[step.strip("*")])

    for h in range(4):
        wait("v", "lk%d" % h, 16)
        n_k = V(g.vector.quantize_mx(words(T.kc, h), words(T.kx, h), T.kt[:, 512 * h:512 * h + 512]))

    n_S, n_A, n_r, n_c, n_e, n_xs, n_xv, n_P, n_pq, n_a, n_v, n_h, n_t = ({} for _ in range(13))
    acc = {"adds": 0}

    def on(k):
        return "v" if "n%s" % k in plan["v"].split() else "s"

    def groups(q, k):
        return sorted(int(t[3:]) for t in plan[q].split() if t[:2] == "x%s" % k)

    def scores(k):
        return T.ps[:, 512 * k:512 * k + 512]

    def t_S(k):
        wait("t", "vv", n_k)
        if k != OWN_:
            wait("t", "qa%d" % order[k], ne)
            wait("t", "qb%d" % order[k], ne)
        n_S[k] = M(g.tensor.matmul_mx(scores(k), words(T.qc, k), words(T.qx, k), T.kc[:], T.kx[:], True, True))

    def v_r(k):
        wait("v", "tt", n_S[k])
        n_r[k] = V(g.vector.tensor_reduce(T.rm[:, k:k + 1], scores(k), AX, Op.max, negate=True))

    def cneg(k):
        return T.cn[:, order[k]:order[k] + 1]

    def v_n(k):
        wait("v", "vv", n_r[k])
        n_c[k] = ("vv", V(g.vector.tensor_scalar(cneg(k), T.rm[:, k:k + 1], SCALE, None, Op.mult)))

    def s_n(k):
        wait("s", "vv", n_r[k])
        n_c[k] = ("ss", E(g.scalar.activation(cneg(k), T.rm[:, k:k + 1], Fn.Copy, scale=SCALE)))

    def s_e(k):
        wait("s", *n_c[k])
        n_e[k] = E(g.scalar.activation(T["en%d" % k][:, :, :], scores(k), Fn.Exp, bias=cneg(k), scale=SCALE))

    def block(buf, part, col):
        return buf[32 * part:32 * part + 32, :, 32 * col:32 * col + 32]

    def s_x(k, kk):
        wait("s", "ss", n_e[k])
        for a in range(4):
            n_xs[k] = E(g.scalar.activation(block(T["et%d" % k], kk, a), block(T["en%d" % k], a, kk), Fn.Copy))

    def v_x(k, kk):
        wait("v", "ss", max(n_fl, n_e[k]))
        for a in range(4):
            n_xv[k] = V(g.vector.tensor_scalar(block(T["et%d" % k], kk, a), block(T["en%d" % k], a, kk),
                                               T.fl[32 * a:32 * a + 32, 0:1], None, Op.max))

    def v_c(k):
        wait("v", "ss", n_xs[k])
        n = len(groups("s", k))
        for lo, hi in ((0, min(n, 2)), (2, n)):
            if lo < hi:
                carried = T["et%d" % k][32 * lo:32 * hi, :, :]
                n_xv[k] = V(g.vector.tensor_scalar(carried, carried, T.fl[32 * lo:32 * hi, 0:1], None, Op.max))

    def v_p(k):
        wait("v", "vv", n_xv[k])
        P = T["p%d" % k]
        for b in range(4):
            n_P[k] = V(g.vector.transpose(P[:, b:512:4], T["et%d" % k][:, b, :]))
        wait("v", "vv", n_P[k])
        n_pq[k] = V(g.vector.quantize_mx(words(T.pc, k), words(T.px, k), P[:]))

    def y_P(k):
        wait("y", "vv", n_P[k])
        g.sync.dma_start(T.p[order[k]], T["p%d" % k][:]).then_inc(S.out, 16)

    def v_v(_k):
        wait("v", "lv", 16)
        n_v[0] = V(g.vector.quantize_mx(words(T.vc, 0), words(T.vx, 0), T.vt[:]))

    def t_A(k):
        wait("t", "vv", max(n_pq[k], n_v[0]))
        n_A[k] = M(g.tensor.matmul_mx(T.pa[:, 512 * k:512 * k + 256], words(T.pc, k), words(T.px, k), T.vc[:], T.vx[:],
                                      True, True))

    def s_a(k):
        wait("s", "tt", n_A[k])
        n_a[k] = E(g.scalar.activation(T["st%d" % k][:], T.pa[:, 512 * k:512 * k + W], Fn.Copy))

    def v_W(_k):
        wait("v", *n_c[OWN_])
        n = V(g.vector.tensor_copy(shift_of(rank), cneg(OWN_)))
        wait("v", "cp", ne)
        wait("v", "cyl", 2 * ne)
        wait("v", "vv", n)
        n_t["W"] = V(g.vector.tensor_reduce(T.mn[:, 0:1], T.cl[:, 0:16:4], AX, Op.min))

    def s_w(_k):
        wait("s", "vv", n_t["W"])
        n_t["w"] = E(g.scalar.activation(T.cw[:, 4:8], T.cl[:, 0:16:4], Fn.Exp, bias=T.mn[:, 0:1], scale=-1.0))

    def v_U(_k):
        for k in range(4):
            wait("v", *n_c[k])
        n = V(g.vector.tensor_scalar(T.cw[:, 0:4], T.cn[:, 0:4], -1.0, None, Op.mult))
        wait("v", "ss", n_t["w"])
        wait("v", "vv", n)
        n_t["U"] = V(g.vector.transpose(T.cwt[:], T.cw[:]))

    def y_U(_k):
        wait("y", "vv", n_t["U"])
        for a in range(4):
            g.sync.dma_start(T.c[:, 32 * a:32 * a + 32], T.cwt[32 * a:32 * a + 4, :]).then_inc(S.out, 16)
            g.sync.dma_start(T.w[:, 32 * a:32 * a + 32], T.cwt[32 * a + 4:32 * a + 8, :]).then_inc(S.out, 16)

    last = [int(t[1]) for t in plan["v"].split() if t[0] == "h"][-1]

    def weight(k):
        return T.cw[:, 4 + order[k]:5 + order[k]]

    def width(k):
        return 128 if k == last else W

    def s_h(k):
        wait("s", "ss", n_t["w"])
        if k == OWN_:
            wait("s", "tt", n_A[k])
            src = T.pa[:, 512 * k:512 * k + width(k)]
        else:
            wait("s", "am%d" % order[k], ne)
            src = T["al%d" % k][:, 0:width(k)]
        n_h[k] = E(g.scalar.activation(T["nu%d" % k][:, 0:width(k)], src, Fn.Copy, scale=weight(k)))

    def v_h(k):
        if "at" not in acc:
            acc["at"], acc["n"] = T["nu%d" % k], ("ss", n_h[k])
            return
        if k == last:
            wait("v", "ss", n_t["w"])
            wait("v", "am%d" % order[k], ne)
            wait("v", *acc["n"])
            n = V(g.vector.tensor_scalar(T.dn[:, 0:1], T["al%d" % k][:, 128:129], weight(k), acc["at"][:, 128:129],
                                         Op.mult, Op.add))
            wait("v", "vv", n)
            V(g.vector.reciprocal(T.ri[:, 0:1], T.dn[:, 0:1]))
        wait("v", *acc["n"])
        wait("v", "ss", n_h[k])
        acc["adds"] += 1
        to, n = T["ac%d" % acc["adds"]], width(k)
        acc["n"] = ("vv", V(g.vector.tensor_tensor(to[:, 0:n], acc["at"][:, 0:n], T["nu%d" % k][:, 0:n], Op.add)))
        acc["at"] = to

    steps = {"tS": t_S, "tA": t_A, "vr": v_r, "vn": v_n, "sn": s_n, "vx": v_x, "vc": v_c, "vp": v_p, "vv": v_v, "se": s_e,
             "sx": s_x, "sa": s_a, "vW": v_W, "sw": s_w, "vU": v_U, "sh": s_h, "vh": v_h, "yP": y_P, "yU": y_U}

    def needs(q, t):
        kind, k = q + t[0], t[1:2]
        if kind == "vc":
            return ["sx%s:%d" % (k, x) for x in groups("s", k)]
        if kind == "vp":
            return ["vx%s:%d" % (k, x) for x in groups("v", k)] + (["vc" + k] if groups("s", k) else [])
        if kind == "vU":
            return ["sw"] + [on(j) + "n%d" % j for j in range(4)]
        return {"tS": [], "vv": [], "vr": ["tS" + k], "vn": ["vr" + k], "sn": ["vr" + k], "se": [on(k) + "n" + k],
                "sx": ["se" + k], "vx": ["se" + k], "tA": ["vp" + k, "vv"], "sa": ["tA" + k], "vW": [on(OWN_) + "n0"],
                "sw": ["vW"], "sh": ["sw"] + (["tA0"] if k == "0" else []), "vh": ["sh" + k], "yP": ["vp" + k],
                "yU": ["vU"]}[kind]

    todo = {q: plan[q].split() for q in "tvsy"}
    done = set()
    while any(todo.values()):
        left = sum(len(x) for x in todo.values())
        for q in "tvsy":
            while todo[q]:
                t = todo[q][0]
                if not all(d in done for d in needs(q, t)):
                    break
                steps[q + t[0]](*([int(x) for x in t[1:].split(":")] if t[1:] else [0]))
                done.add(q + t)
                todo[q].pop(0)
        if left == sum(len(x) for x in todo.values()):
            raise ValueError("the queues' orders wait for one another in a ring")

    def road(k, what):
        if k == PAR_:
            return (cores[PAR],) + ((shift_of(rank), "cp") if what == "c" else (land(PAR, rank), "am%d" % rank))
        if is_gate:
            r = order[k]
            return (cores[r],) + ((shift_of(rank), "cyl") if what == "c" else (land(r, rank), "am%d" % rank))
        if what == "c":
            return (helper,) + ((T.fc[:, 0:1], "rcx") if k == X_ else (T.fc[:, 4:5], "rcy"))
        return (helper,) + ((T.fx[:], "rx") if k == X_ else (T.fy[:], "ry"))

    for s in plan["sends"].split():
        k = int(s[1])
        if s[0] == "c":
            wait("g", *n_c[k])
            send(cneg(k), *road(k, "c"))
        else:
            wait("g", "ss", n_a[k])
            send(T["st%d" % k][:], *road(k, "A"))

    wait("s", *acc["n"])
    wait("v", *acc["n"])
    for i in range(16):
        a, d = i // 4, i % 4
        out, src = T.rt[32 * d:32 * d + 32, 32 * a:32 * a + 32], acc["at"][32 * a:32 * a + 32, 32 * d:32 * d + 32]
        by = T.ri[32 * a:32 * a + 32, 0:1]
        if i < TAIL_SCALAR:
            ns = E(g.scalar.activation(out, src, Fn.Copy, scale=by))
        else:
            n = V(g.vector.tensor_scalar(out, src, by, None, Op.mult))
    wait("v", "ss", ns)
    wait("v", "vv", n)
    n = V(g.vector.transpose(T.res[:], T.rt[:]))
    wait("y", "vv", n)
    g.sync.dma_start(T.o[:], T.res[:]).then_inc(S.out, 16)
    g.sync.wait_ge(S.out, 16 * 13)
    wait("g", "ss", tick["ss"])
    wait("g", "tt", tick["tt"])
    wait("g", "ls", sent[0])
